import numpy as np, ml_dtypes
CORES = [1,5,17,21,33,37,49,53]
N = 8
BF = ml_dtypes.bfloat16
def gentries(a):
    return np.ascontiguousarray(a.reshape(8, 16, -1).transpose(0, 2, 1)).reshape(8, -1)
def gtable(e):
    e = np.asarray(e); return np.ascontiguousarray(e.reshape(8, -1, 16).transpose(0, 2, 1)).reshape(128, -1).astype(np.int32)
V, RO, HOP = 1024, 2, 1
W = N * V
def rings(o, cut):
    t = np.arange(W); c = cut.copy(); c[0] = True
    first = np.maximum.accumulate(np.where(c, t, 0)); nt = np.where(np.append(c[1:], True), first, t + 1)
    nx = np.empty(W, np.int64); pv = np.empty(W, np.int64); nx[o] = o[nt]; pv[o[nt]] = o
    return nx, pv
def walk(rng, n, step):
    w = np.add.accumulate(rng.integers(-step, step + 1, (16, n)), axis=1) + rng.integers(0, 256, (16, 1))
    return np.abs((w + 255) % 510 - 255)
def curve(rng, o, step, off, slide, share):
    h = W // 2; a = walk(rng, h, step); t = np.arange(h)
    xs = np.empty((16, W), np.int64); xs[:, o[:h]] = a; xs[:, o[h:]] = np.clip(a + rng.integers(-off, off + 1, (16, h)), 0, 255)
    cut = rng.random(W) < share
    if share >= 0: cut[h] = True; cut[0:16:3] = True
    nx, pv = rings(o, cut); s = rng.integers(-slide, slide + 1, (2, h)); p = np.empty(W, np.int64)
    p[o[:h]] = o[h + (t + s[0]) % h]; p[o[h:]] = o[(t + s[1]) % h]
    return xs, nx, pv, p
def odd(rng, o, nx, pv, p):
    m = rng.random(W)
    p = np.where(m < 0.03, rng.integers(0, W, W), np.where(m < 0.05, np.arange(W), np.where(m < 0.07, nx, np.where(m < 0.09, pv, p))))
    p[o[0:15:3]] = nx[o[0:15:3]]; p[o[1:15:3]] = pv[o[1:15:3]]
    return p
def links(a):
    return np.stack([gtable(a.reshape(8, N, V)[:, q]) for q in range(N)])
def pack(gs, th):
    xs, nx, pv, p = [np.stack(a) for a in zip(*gs)]
    return {"x": np.ascontiguousarray(xs.reshape(8, 16, N, V).transpose(2, 0, 1, 3)).reshape(N, 128, V).astype(np.int32),
            "nxt": links(nx), "prv": links(pv), "ptn": links(p),
            "th": np.tile(np.repeat(np.asarray(th), 16)[None, :, None], (N, 1, 1)).astype(np.int32)}
def setup_inputs(rng):
    gs, th = [], []
    for g in range(8):
        off = int(rng.integers(4, 13)); step = int(rng.integers(off, 2 * off + 1)); o = rng.permutation(W)
        xs, nx, pv, p = curve(rng, o, step, off, RO, 0.02)
        gs.append((xs, nx, pv, odd(rng, o, nx, pv, p))); th.append(int(rng.integers(4 * off * off, 9 * off * off)))
    return pack(gs, th)
def setup_inputs_ties(rng):
    gs, th = [], []; w = np.arange(W)
    for g in range(8):
        o = rng.permutation(W)
        if g == 6: o = np.ascontiguousarray(w.reshape(N, 2, V // 2).transpose(1, 0, 2)).reshape(-1)
        if g == 7: o = w
        q = int(rng.integers(1, 5)); xs, nx, pv, p = curve(rng, o, 4, 0, 1, -1.0 if g == 5 else 0.02)
        sort = rng.integers(0, 3, W) if g > 1 else np.zeros(W, np.int64)
        u = rng.integers(0, 250, (16, 1)); lo = np.arange(16)[:, None] < 8
        xs = u + q * np.where(sort == 1, lo, np.where(sort == 2, ~lo, False)).astype(np.int64)
        gs.append((xs, nx, pv, p)); th.append((1, 0, 8 * q * q, 8 * q * q + 1, 16 * q * q, 16 * q * q + 1, 8 * q * q, 8 * q * q + 1)[g])
    return pack(gs, th)
def setup_inputs_loops(rng):
    gs, th = [], []; ra, rb, rc = [int(v) for v in rng.permutation(N)[:3]]; w = np.arange(W).reshape(N, V); k = V // 2; c = W - 2 * V; b = W - V
    for g in range(8):
        out = [q for q in range(N) if q != rb and q != rc and (g < 7 or q != ra)]
        few = w[ra] if g == 7 else w[ra][:0]
        o = np.concatenate([rng.permutation(w[out].reshape(-1)), rng.permutation(few), rng.permutation(w[rc]), rng.permutation(w[rb])])
        m = len(out) * V; h = m // 2; t = np.arange(h); j = np.arange(c - m) % 6
        xs = np.empty((16, W), np.int64); xs[:, o] = walk(rng, W, 6)
        xs[:, o[h:m]] = np.clip(xs[:, o[:h]] + rng.integers(-4, 5, (16, h)), 0, 255)
        xs[:, o[c + k:b]] = np.clip(xs[:, o[c:c + k]] + rng.integers(-4, 5, (16, k)), 0, 255)
        cut = rng.random(W) < (1.0, -1.0, 0.5, 0.3, 0.4, 0.05, 0.02, 0.3)[g]
        if g != 1: cut[h] = True
        cut[m] = True; cut[m:c] = (j == 0) | (j == 3) | (j == 5); cut[c:b] = True; cut[b] = True
        if g == 6: cut[1:16] = False
        nx, pv = rings(o, cut); s = rng.integers(-1, 2, (2, h)); p = np.empty(W, np.int64)
        p[o[:h]] = o[h + (t + s[0]) % h]; p[o[h:m]] = o[(t + s[1]) % h]
        i = o[m:c]; u = rng.integers(0, 3, c - m); p[i] = np.where(u == 0, i, np.where(u == 1, nx[i], pv[i]))
        p[o[c:c + k]] = o[c + k:b]; p[o[c + k:b]] = o[c:c + k]; p[o[b:]] = o[rng.integers(0, m, V)]
        if 2 <= g <= 4:
            i = o[0:m:2]; p[i] = np.where(rng.random(h) < 0.7, nx[i], p[i])
            i = o[1:m:2]; p[i] = np.where(rng.random(h) < 0.7, pv[i], p[i])
        if g == 5: p = ra * V + rng.integers(0, V, W)
        if g == 6:
            u = rng.integers(60, 196, (16, 1)); xs = u + rng.integers(-40, 41, (16, W))
            xs[:, o[np.array([5, 20])]] = u; xs[:, o[np.array([3, 4, 6, 7])]] = np.where(u < 128, 255, 0)
            p = np.full(W, o[5], np.int64); p[o[5]] = o[20]
        if g == 7:
            i = o[:m]; p[i] = np.where(rng.random(m) < 0.75, i, p[i])
        gs.append((xs, nx, pv, p)); th.append(10000 if g == 6 else int(rng.integers(300, 4000)))
    return pack(gs, th)
def setup_inputs_ends(rng):
    gs, th = [], []; h = W // 2
    for g in range(8):
        r = 1 + rng.permutation(W - 2); o = np.concatenate([np.array([0]), r[:h - 1], np.array([W - 1]), r[h - 1:]])
        xs, nx, pv, p = curve(rng, o, 4, 0, 0, 0.02)
        if g == 0: p[o[3:15:3]] = nx[o[3:15:3]]; p[o[4:15:3]] = pv[o[4:15:3]]
        xs = 255 * rng.integers(0, 2, (16, W))
        if g == 1:
            nx, pv = rings(o, np.arange(W) % 4 == 0); y = 255 * rng.integers(0, 2, (16, W // 4, 2)); s = rng.integers(0, 3, W)
            xs[:, o] = np.concatenate([y, 255 - y], axis=2).reshape(16, W); p = np.where(s == 0, nx, np.where(s == 1, pv, nx[nx]))
        if g in (2, 3, 7):
            u = 255 * rng.integers(0, 2, (16, 1)); xs[:, o[:h]] = u; xs[:, o[h:]] = 255 - u
        if g == 7: xs[14] = 100; xs[15] = 100 + rng.integers(0, 2, W)
        gs.append((xs, nx, pv, p)); th.append((2 ** 20, 2 ** 20, 1040400, 1040401, 520200, 0, 1, 14 * 255 * 255 + 1)[g])
    return pack(gs, th)
def setup_inputs_near(rng):
    gs, th = [], []; h = W // 2; back = int(rng.integers(0, 2))
    for g in range(8):
        r = np.stack([q * V + rng.permutation(V) for q in range(N)])
        o = np.concatenate([np.ascontiguousarray(r[:, :V // 2].T).reshape(-1), np.ascontiguousarray(np.roll(r[:, V // 2:], N // 2, axis=0).T).reshape(-1)])
        off = int(rng.integers(2, 6)); a = walk(rng, h, 16 * off)
        xs = np.empty((16, W), np.int64); xs[:, o[:h]] = a; xs[:, o[h:]] = np.clip(a + rng.integers(-off, off + 1, (16, h)), 0, 255)
        cut = (rng.random(W) < 0.04) & (np.arange(W) % N == 0); cut[h] = True
        nx, pv = rings(o, cut); mate = np.empty(W, np.int64); mate[o[:h]] = o[h:]; mate[o[h:]] = o[:h]
        gs.append((xs, nx, pv, pv[mate] if back else nx[mate])); th.append(int(rng.integers(17 * off * off, 40 * off * off)))
    return pack(gs, th)
def setup_inputs_spread(rng):
    gs, th = [], []
    for g in range(8):
        o = rng.permutation(W); xs, nx, pv, p = curve(rng, o, int(rng.integers(2, 40)), int(rng.integers(0, 30)), RO, 0.02)
        xs = np.where(rng.random(W) < 0.1, rng.integers(0, 256, (16, W)), xs >> rng.integers(0, 7, (16, 1)))
        gs.append((xs, nx, pv, odd(rng, o, nx, pv, p))); th.append(int(2.0 ** (20 * rng.random())))
    return pack(gs, th)
def joined(a):
    return np.ascontiguousarray(np.stack([gentries(b) for b in a]).transpose(1, 0, 2)).reshape(8, W).astype(np.int64)
def check_inputs(d):
    bad = []
    for k, hi in (("x", 255), ("nxt", W - 1), ("prv", W - 1), ("ptn", W - 1), ("th", 2 ** 20)):
        if np.min(d[k]) < 0 or np.max(d[k]) > hi: bad.append("range of " + k)
    t = d["th"].reshape(N, 8, 16)
    if np.any(t != t[:1, :, :1]): bad.append("th alike on all ranks and in a group")
    if "range of nxt" not in bad and "range of prv" not in bad:
        if np.any(np.take_along_axis(joined(d["prv"]), joined(d["nxt"]), 1) != np.arange(W)[None, :]): bad.append("prv is the inverse of nxt")
    return bad
def at(a, i):
    return np.take_along_axis(a, i, 1)
def points(a, i):
    return np.take_along_axis(a, i[:, None, :], 2)
def reference(x, nxt, prv, ptn, th):
    z = np.ascontiguousarray(x.astype(np.int64).reshape(N, 8, 16, V).transpose(1, 2, 0, 3)).reshape(8, 16, W)
    nx = joined(nxt); pv = joined(prv); p = joined(ptn); t = th[0].astype(np.int64).reshape(8, 16)[:, :1]
    me = np.arange(W)[None, :]
    for rnd in range(RO):
        a = at(nx, p); b = at(pv, p)
        c = np.stack([p, a, b] + ([at(nx, a), at(pv, b)] if HOP == 2 else []))
        d = np.stack([np.add.reduce((z - points(z, k)) ** 2, axis=1) for k in c])
        d = np.where((c == me) | (c == nx) | (c == pv), 2 ** 21, d)
        k = np.argmin(d, axis=0)[None]
        p = np.take_along_axis(c, k, 0)[0]; e = np.take_along_axis(d, k, 0)[0]
        swap = (at(p, p) == me) & (e < t)
        nx, pv = np.where(swap, at(nx, p), nx), np.where(at(swap, pv), at(p, pv), pv)
        z = (2 * z + points(z, nx) + points(z, pv)) >> 2
    return {"yx": np.ascontiguousarray(z.reshape(8, 16, N, V).transpose(2, 0, 1, 3)).reshape(N, 128, V).astype(np.float32),
            "yn": links(nx).astype(np.float32), "yv": links(pv).astype(np.float32), "yp": links(p).astype(np.float32)}

@@ -1,0 +1,547 @@
+from concourse.bass import DstId, RemoteDMATransfer
+from concourse.mybir import AluOpType, ActivationFunctionType
+
+F, B, I, U, H = "float32", "bfloat16", "int32", "uint16", "float16"
+SCRATCH = {}
+for _d, _names in {
+    I: "xi:1024 pi:8 thi:4 thb:4 la:192 pb:64 ti:256",
+    B: "sx:1024 land:1024 xa:1024 gn:1024 xt0:8192 xt1:8192 df:3072 rep:1024 xrep:1024 gm:2304 idn:256 i128:128 i1:128 "
+       "i8:128 jj:144 ah:192 al:192 abh:128 abl:128 wh:64 wl:64 dhl:128 dha:128 thl:128",
+    F: "uu:1024 sq:3072 gp:1024 m8:1024 m16:1024 lt:1024 wt:1024 dtab:512 ft:1536 pu:16 pvv:8 i16:16 i16b:16 pf:8 cc:8 "
+       "fl0:12 fl1:8 pj0:8 ida0:128 ida:128 idb:64 sel:32 t8:8 t16:16 thf:4 af:192 bfl:192 abp:128 abb:128 ee:192 uv:128 "
+       "pen:192 s1:512 eqp:64 nwp:64 ww:64",
+    U: "flo:12 flp:8 pjo:8 op:64 oab:128 olo:64 ohi:64 vlo:64 vhi:64 on:64 ov:64",
+    H: "v16:1024",
+}.items():
+    for _w in _names.split():
+        SCRATCH[_w.split(":")[0]] = ("sbuf", [128, int(_w.split(":")[1])], _d)
+for _n, _w, _d in [("l", 16, I), ("p", 8, I), ("o", 16, F), ("v", 8, F), ("x0", 64, B), ("x1", 64, B)]:
+    SCRATCH["d" + _n] = ("dram", [8, 128, _w], _d)
+    SCRATCH["land" + _n] = ("dram", [8, 128, _w], _d)
+for _k in range(8):
+    SCRATCH["ps%d" % _k] = ("psum", [128, 512], F)
+SEMAPHORES = (["cv", "cs", "cp", "cg"] + ["d%d" % k for k in range(60)] + ["arl", "arp", "aro", "arv", "arx0", "arx1", "arm"]
+              + ["ar%d" % k for k in range(1, 4)] + ["sn%d" % k for k in range(10)])
+
+CH = [(0, 512), (512, 768), (768, 1024)]
+HV = [(0, 512), (512, 1024)]
+
+
+def rank_program(g, core, T, topo):
+    r = T.rank_of(core)
+    if r is None:
+        return
+    cores = list(T.cores)
+    ops = []
+    Q = {"v": g.vector, "s": g.scalar, "p": g.tensor, "g": g, "y": g.sync}
+    Alu, Act = AluOpType, ActivationFunctionType
+
+    def A(name, c0=None, c1=None, st=None, p0=0, p1=128):
+        t = T[name]
+        if c0 is None:
+            c0, c1 = 0, t.shape[1]
+        ap = t[p0:p1, c0:c1:st] if st else t[p0:p1, c0:c1]
+        return ap, [(name, p0, p1, c0, c1)]
+
+    def D(name, k=None, t=None):
+        b = T[name]
+        if t is None:
+            ap = b[:] if k is None else b[k]
+        else:
+            ap = b[:, 64 * t:64 * t + 64, :] if k is None else b[k, 64 * t:64 * t + 64, :]
+        return ap, [(name, 0 if k is None else k, 8 if k is None else k + 1, 0 if t is None else t, 4 if t is None else t + 1)]
+
+    def X(ap):
+        return ap, []
+
+    def IND(win, off, c0=0, c1=1024, w1=None):
+        w, o = (A(win) if w1 is None else A(win, 0, w1)), A(off, c0 // 16, c1 // 16)
+        return w[0].indirect(o[0]), w[1] + o[1]
+
+    def add(q, fn, outs, ins, kind="c", sem=None, n=0):
+        ops.append({"q": q, "fn": fn, "w": [k for o in outs for k in o[1]], "r": [k for o in ins for k in o[1]],
+                    "kind": kind, "sem": sem, "n": n})
+
+    def col(s):
+        return [s] if isinstance(s, tuple) else []
+
+    def val(s):
+        return s[0] if isinstance(s, tuple) else s
+
+    def tt(o, a, b, op):
+        add("v", lambda: g.vector.tensor_tensor(o[0], a[0], b[0], op), [o], [a, b])
+
+    def ts(o, a, s1, op0, s2=None, op1=None):
+        if op1 is None:
+            add("v", lambda: g.vector.tensor_scalar(o[0], a[0], val(s1), None, op0), [o], [a] + col(s1))
+        else:
+            add("v", lambda: g.vector.tensor_scalar(o[0], a[0], val(s1), val(s2), op0, op1), [o], [a] + col(s1) + col(s2))
+
+    def cp(o, a, q="v"):
+        if q == "v":
+            add("v", lambda: g.vector.tensor_copy(o[0], a[0]), [o], [a])
+        else:
+            add("s", lambda: g.scalar.activation(o[0], a[0], Act.Copy), [o], [a])
+
+    def act(o, a, f, bias=0.0, scale=1.0):
+        add("s", lambda: g.scalar.activation(o[0], a[0], f, bias=bias, scale=scale), [o], [a])
+
+    def mm(o, l, m, st, sp):
+        add("p", lambda: g.tensor.matmul(o[0], l[0], m[0], st, sp), [o], [l, m])
+
+    def iota(o, pat, base, cm, flt=True):
+        if flt:
+            add("g", lambda: g.iota(o[0], pat, base, cm, allow_small_or_imprecise_dtypes=True), [o], [])
+        else:
+            add("g", lambda: g.iota(o[0], pat, base, cm), [o], [])
+
+    nd = [0]
+
+    def dma(q, o, a):
+        sem = "d%d" % nd[0]
+        nd[0] += 1
+        add(q, lambda: Q[q].dma_start(o[0], a[0]), [o], [a], "d", sem, 16)
+
+    ns = [0]
+
+    def bits(es):
+        return sum(1 << e for e in es)
+
+    def send(items):
+        sem = "sn%d" % ns[0]
+        ns[0] += 1
+        trs = []
+        for q, es, src, dst, rs in items:
+            rid, pid, _ = topo.addr(cores[q])
+            trs.append(RemoteDMATransfer(dst_ids=[DstId(rid=rid, pnc=pid)], dma_engine_mask=bits(es),
+                                         remote_sem=T.sem[rs], src=src[0], dst=dst))
+        add("g", lambda: g.remote_dma_fused(trs, local_sem=T.sem[sem]), [], [i[2] for i in items], "r", sem,
+            sum(len(i[1]) for i in items))
+
+    def arrive(outs, sem, n):
+        add(None, None, outs, [], "a", sem, n)
+
+    chips = sorted(set(topo.chip(c) for c in cores))
+    on = [[q for q in range(8) if topo.chip(cores[q]) == ch] for ch in chips]
+    ci = chips.index(topo.chip(core))
+    mate = [q for q in on[ci] if q != r][0]
+    to = [None] + [on[(ci + k) % 4] for k in (1, 2, 3)]
+    fr = [None] + [on[(ci - k) % 4] for k in (1, 2, 3)]
+    far = topo.engines(core, cores[to[1][0]])
+    near = [e for e in topo.engines(core, cores[mate]) if e not in far]
+    hf = len(far) // 2
+    others = to[1] + to[2] + to[3]
+    solo = far[0::2] + far[1::2]
+
+    def exchange(n):
+        src, dst, sem = "d" + n, "land" + n, "ar" + n
+        send([(mate, near[:2], D(src, mate), T[dst][r], sem)]
+             + [(q, [solo[j]], D(src, q), T[dst][r], sem) for j, q in enumerate(others)])
+        arrive([D(dst, q) for q in range(8) if q != r], sem, 8)
+
+    def P(k, c0=None, c1=None, st=None):
+        return A("ps%d" % k, c0, c1, st)
+
+    def blk(name, k, n=64):
+        return A(name, n * k, n * k + n)
+
+    def S1(k):
+        return blk("s1", k)
+
+    def Z(k):
+        return blk("ps5", k)
+
+    lists = [T.prv, T.nxt, T.ptn]
+    for t in range(3):
+        dma("y" if t % 2 == 0 else "s", D("dl", None, t) if t < 2 else D("dp"), X(lists[t][:]))
+    order = to[1] + [mate] + to[2] + to[3] + [r]
+    for j, q in enumerate(order):
+        dma("s" if j % 2 == 0 else "y", blk("xi", j, 128), X(T.x[16 * q:16 * q + 16, :]))
+    for t in range(3):
+        dma("s", D("landl", r, t) if t < 2 else D("landp", r), X(lists[t][16 * r:16 * r + 16, :]))
+
+    iota(A("i8"), [[0, 8], [8, 16]], 0, 0)
+    iota(A("pvv"), [[-1, 8]], 0, 1)
+    iota(A("pi", 0, 1), [[0, 1]], 0, 1, False)
+    iota(A("i1"), [[0, 8], [1, 16]], 0, 0)
+    iota(A("pu"), [[-8, 16]], 0, 1)
+    iota(A("jj"), [[0, 9], [200, 2], [1, 8]], -200, 0)
+    exchange("l")
+    for k in range(8):
+        ts(blk("xrep", k, 128), A("i8"), A("pvv", k, k + 1), Alu.is_equal)
+    for k, (s1, o0) in enumerate([(7, Alu.bitwise_and), (15, Alu.bitwise_and), (3, Alu.arith_shift_right), (4, Alu.arith_shift_right)]):
+        ts(A("pi", k + 1, k + 2), A("pi", 0, 1), s1, o0)
+    ts(A("pi", 5, 6), A("pi", 0, 1), 3, Alu.arith_shift_right, 1, Alu.bitwise_and)
+    for k in range(8):
+        ts(blk("rep", k, 128), A("i1"), A("pu", 2 * k, 2 * k + 1), Alu.is_equal)
+    cp(A("pf", 0, 6), A("pi", 0, 6))
+
+    def piece(j):
+        return blk("sx", j, 128)
+
+    mine = T.land[:, 128 * r:128 * r + 128]
+    cp(A("sx", 0, 384), A("xi", 0, 384))
+    send([(to[1][0], far[:hf], piece(0), mine, "ar1"), (to[1][1], far[hf:], piece(1), mine, "ar1"),
+          (mate, near, piece(2), mine, "arm")])
+    exchange("p")
+    cp(A("sx", 384, 640), A("xi", 384, 640))
+    send([(to[2][0], far[:hf], piece(3), mine, "ar2"), (to[2][1], far[hf:], piece(4), mine, "ar2")])
+    cp(A("sx", 640, 896), A("xi", 640, 896))
+    send([(to[3][0], far[:hf], piece(5), mine, "ar3"), (to[3][1], far[hf:], piece(6), mine, "ar3")])
+    cp(blk("land", r, 128), A("xi", 896, 1024))
+    arrive([blk("land", mate, 128)], "arm", len(near))
+    for k in (1, 2, 3):
+        arrive([blk("land", q, 128) for q in fr[k]], "ar%d" % k, 2 * hf)
+
+    iota(A("i16b"), [[1, 2], [2, 8]], 0, 0)
+    iota(A("i16"), [[1, 16]], 0, 0)
+    iota(A("fl0"), [[512, 3], [16, 4]], 0, 0)
+    iota(A("fl1"), [[512, 2], [2, 4]], 0, 0)
+    iota(A("pj0"), [[64, 2], [2, 4]], 0, 0)
+    iota(A("idb"), [[128, 8], [1024, 8]], 0, 1)
+    iota(A("ida0", 0, 64), [[16, 64]], 0, 1)
+    iota(A("ida0", 64, 128), [[16, 8], [128, 8]], 0, 1)
+    iota(A("i128"), [[1, 128]], 0, 0)
+    dma("g", A("thi", 0, 1, None, 0, 2), X(T.th[16 * r:16 * r + 2, :]))
+    add("g", lambda: g.partition_broadcast(T.thb[:, 0:1], T.thi[0:1, 0:1], 128), [A("thb")], [A("thi")])
+    for k in range(16):
+        ts(blk("gm", k, 144), A("jj"), A("pu", k, k + 1), Alu.is_equal)
+
+    def pf(k):
+        return A("pf", k, k + 1)
+
+    def cc(k):
+        return A("cc", k, k + 1)
+
+    def constants():
+        ts(cc(0), pf(1), 64.0, Alu.mult, pf(4), Alu.add)
+        ts(cc(2), pf(1), 8.0, Alu.mult, pf(5), Alu.add)
+        ts(cc(3), pf(4), 1008.0, Alu.mult)
+        ts(cc(6), pf(4), 8.0, Alu.mult, pf(5), Alu.add)
+        ts(A("sel", 0, 16), A("i16b"), pf(3), Alu.is_equal)
+        ts(cc(1), pf(5), 8.0, Alu.mult, cc(0), Alu.add)
+        ts(cc(7), pf(1), 64.0, Alu.mult, cc(6), Alu.add)
+        ts(A("t8"), A("i16", 0, 8), pf(1), Alu.is_equal)
+        ts(A("t16"), A("i16"), pf(2), Alu.is_equal)
+        tt(A("sel", 16, 24), A("sel", 0, 8), A("sel", 8, 16), Alu.add)
+        ts(A("flp"), A("fl1"), cc(7), Alu.add)
+        ts(A("pjo"), A("pj0"), cc(2), Alu.add)
+        ts(A("ida"), A("ida0"), cc(3), Alu.add)
+        ts(A("flo"), A("fl0"), cc(1), Alu.add)
+        ts(A("sel", 24, 32), A("sel", 16, 24), 2.0 ** -21, Alu.mult)
+        for k, v in enumerate([1.0, 2.0]):
+            ts(blk("idn", k, 128), A("i128"), pf(0), Alu.is_equal, v, Alu.mult)
+
+    ONES, DIST = A("sel", 16, 24), A("sel", 24, 32)
+
+    def conv(src, base, c0, c1, sel, bank, c=0):
+        for b in range(c0 // 128, c1 // 128):
+            mm(P(bank, c + 8 * b, c + 8 * b + 8), A(src, base + 128 * b, base + 128 * b + 128), sel, True, True)
+
+    def conv2(c0, c1, bank):
+        for b in range(c0 // 128, c1 // 128):
+            mm(P(bank, b, 128, 8), A("gp", 128 * b, 128 * b + 128), A("sel", 0, 16), True, True)
+
+    def table16(bank, pts, qs=range(8)):
+        for q in qs:
+            for j, pt in enumerate(pts):
+                mm(P(bank, 64 * q, 64 * q + 64), blk("rep", q, 128), pt, j == 0, j == len(pts) - 1)
+
+    def gmat(u, t):
+        return A("gm", 144 * u + 8 - 8 * t, 144 * u + 136 - 8 * t)
+
+    def link_table(s3, bank, e):
+        for q in range(8):
+            for j, (t, nm) in enumerate([(1, "ah"), (1, "al"), (0, "ah"), (0, "al")]):
+                mm(P(bank, 64 * q, 64 * q + 64), gmat(2 * q + s3, t), blk(nm, t), j == 0, j == 3)
+        cp(A("lt", s3, 1024, 2), P(bank), e)
+
+    def flip_mm(banks, ptss):
+        for bk, pts in zip(banks, ptss):
+            table16(bk, pts)
+
+    def flip_out(banks, out):
+        for j, bk in enumerate(banks):
+            cp(blk("ft", j, 512), P(bk), "s")
+        n = len(banks)
+        cp(out, IND("ft", "flo", 0, 64 * n, 512 * n), "s")
+
+    def parts(h, lo, n):
+        return [[blk(h, t), blk(lo, t)] for t in range(n)]
+
+    def link_chunk(k, bank):
+        c0, c1 = CH[k]
+        tt(A("gp", c0, c1), IND("lt", "ohi", c0, c1), A("m8", c0, c1), Alu.mult)
+        conv2(c0, c1, bank)
+
+    def link_lists(bank):
+        cp(A("abh"), P(bank, 0, 128))
+        tt(A("abl"), P(bank, 0, 128), A("abh"), Alu.subtract)
+        cp(A("abp"), P(bank, 0, 128))
+
+    def closed():
+        tt(Z(0), A("pb"), A("idb"), Alu.is_equal)
+        tt(blk("ee", 1), A("pb"), blk("bfl", 1), Alu.is_equal)
+        tt(blk("ee", 2), A("pb"), blk("bfl", 0), Alu.is_equal)
+        tt(Z(2), Z(0), blk("ee", 1), Alu.max)
+        tt(Z(3), Z(0), blk("ee", 2), Alu.max)
+        cp(blk("ti", 2), blk("bfl", 0))
+        tt(blk("pen", 0), Z(3), blk("ee", 1), Alu.max)
+        ts(blk("ti", 0), blk("ti", 2), 15, Alu.bitwise_and)
+        tt(blk("uv", 0), blk("abb", 0), blk("bfl", 1), Alu.is_equal)
+        cp(A("vlo"), blk("ti", 0))
+        tt(blk("uv", 1), blk("abb", 1), blk("bfl", 0), Alu.is_equal)
+        tt(S1(0), blk("abb", 1), A("pb"), Alu.subtract)
+        tt(A("pen", 64, 192), A("ps5", 128, 256), A("uv"), Alu.max)
+
+    nb = [0]
+
+    def points(qs, es):
+        for q in qs:
+            for hh in range(2):
+                bk = 2 + nb[0] % 3
+                for vh in range(4 * hh, 4 * hh + 4):
+                    mm(P(bk, 128 * (vh % 4), 128 * (vh % 4) + 128), blk("xrep", vh, 128), blk("land", q, 128), True, True)
+                cp(blk("xt0", 2 * q + hh, 512), P(bk), es[nb[0] % len(es)])
+                nb[0] += 1
+
+    points([r], "s")
+    constants()
+    points([mate] + fr[1], "sv")
+    for t in range(3):
+        dma("y", blk("la", t), D("landl", None, t) if t < 2 else D("landp"))
+    for q in [r, mate] + fr[1] + fr[2] + fr[3]:
+        dma("y", A("xa", 0, 1024, None, 16 * q, 16 * q + 16), blk("land", q, 128))
+    points(fr[2][:1], "s")
+    cp(A("ah", 0, 128), A("la", 0, 128))
+    tt(A("al", 0, 128), A("la", 0, 128), A("ah", 0, 128), Alu.subtract)
+    ts(blk("ti", 0), blk("la", 2), 7, Alu.bitwise_and)
+    ts(blk("ti", 1), blk("la", 2), 3, Alu.arith_shift_right)
+    cp(A("olo"), blk("ti", 0))
+    points(fr[2][1:], "s")
+    cp(A("m8"), IND("t8", "olo"), "s")
+    cp(blk("ah", 2), blk("la", 2))
+    cp(A("op"), blk("la", 2))
+    tt(blk("al", 2), blk("la", 2), blk("ah", 2), Alu.subtract)
+    cp(A("ohi"), blk("ti", 1))
+    cp(A("af", 0, 128), A("la", 0, 128))
+    ts(A("thf", 0, 1), A("thb", 0, 1), 2.0 ** -21, Alu.mult)
+    link_table(0, 0, "v")
+    link_table(1, 1, "v")
+    points(fr[3], "s")
+    for k in range(3):
+        link_chunk(k, 0)
+    link_lists(0)
+
+    for rnd in range(2):
+        xt = "xt%d" % rnd
+        flip_mm([3, 2], parts("abh", "abl", 2)[::-1])
+        cp(blk("ft", 1, 512), P(3), "s")
+        cp(blk("ft", 0, 512), P(2), "s")
+        tt(A("df", 0, 1024), IND(xt, "op"), A("xa"), Alu.subtract)
+        if rnd == 0:
+            cp(A("oab"), IND("ft", "flp", 0, 128, 1024))
+            cp(A("abb"), IND("abp", "pjo", 0, 128), "s")
+            flip_mm([6, 7, 2], parts("ah", "al", 3))
+            flip_out([6, 7, 2], A("bfl"))
+        else:
+            cp(A("abb"), IND("ft", "flp", 0, 128, 1024), "s")
+        tt(A("df", 1024, 2048), IND(xt, "oab", 1024, 2048), A("xa"), Alu.subtract)
+        act(A("sq", 0, 1024), A("df", 0, 1024), Act.Square)
+        conv("sq", 0, 0, 1024, DIST, 0)
+        act(A("sq", 1024, 2048), A("df", 1024, 2048), Act.Square)
+        conv("sq", 1024, 0, 1024, DIST, 0, 64)
+        for c0, c1 in CH:
+            tt(A("df", 2048 + c0, 2048 + c1), IND(xt, "oab", c0, c1), A("xa", c0, c1), Alu.subtract)
+            if c0 == 0:
+                if rnd == 0:
+                    cp(A("pb"), blk("bfl", 2))
+                closed()
+            act(A("sq", 2048 + c0, 2048 + c1), A("df", 2048 + c0, 2048 + c1), Act.Square)
+            conv("sq", 2048, c0, c1, DIST, 1)
+        tt(S1(1), P(0, 0, 64), blk("pen", 0), Alu.max)
+        tt(Z(0), P(0, 64, 128), blk("pen", 2), Alu.max)
+        tt(Z(1), Z(0), S1(1), Alu.is_lt)
+        tt(S1(2), Z(0), S1(1), Alu.min)
+        tt(Z(2), Z(1), S1(0), Alu.mult)
+        tt(Z(3), Z(2), A("pb"), Alu.add)
+        tt(Z(4), P(1, 0, 64), blk("pen", 1), Alu.max)
+        tt(S1(5), Z(3), blk("abb", 0), Alu.subtract)
+        tt(Z(5), Z(4), S1(2), Alu.is_lt)
+        cp(S1(4), Z(3))
+        tt(S1(7), Z(4), S1(2), Alu.min)
+        tt(Z(6), Z(5), S1(5), Alu.mult)
+        ts(Z(7), S1(7), A("thf", 0, 1), Alu.is_ge, 8192.0, Alu.mult)
+        tt(A("pb"), S1(4), Z(6), Alu.subtract)
+        tt(Z(0), Z(7), blk("bfl", 0), Alu.subtract)
+        ts(blk("ti", 0), A("pb"), 7, Alu.bitwise_and)
+        tt(A("ww"), Z(0), A("pb"), Alu.add)
+        cp(A("olo"), blk("ti", 0))
+        cp(A("wh"), IND("ww", "pjo", 0, 64))
+        cp(A("m8"), IND("t8", "olo"), "s")
+        ts(blk("ti", 1), A("pb"), 3, Alu.arith_shift_right)
+        tt(A("wl"), IND("ww", "pjo", 0, 64), A("wh"), Alu.subtract)
+        tt(Z(1), A("pb"), A("idb"), Alu.subtract)
+        cp(A("ohi"), blk("ti", 1))
+        cp(blk("dhl", 0), Z(1))
+        tt(blk("dhl", 1), Z(1), blk("dhl", 0), Alu.subtract)
+        for s3 in range(2):
+            for h in range(8):
+                mm(P(6 + s3, h, 512, 8), gmat(2 * h + s3, 0), A("wh"), True, False)
+                mm(P(6 + s3, h, 512, 8), gmat(2 * h + s3, 0), A("wl"), False, True)
+            tt(A("wt", s3, 1024, 2), P(6 + s3), A("lt", s3, 1024, 2), Alu.add)
+        flip_mm([2, 3], [[blk("dhl", 0)], [blk("dhl", 1)]])
+        flip_out([2, 3], A("dha"))
+        for c0, c1 in CH:
+            tt(A("gp", c0, c1), IND("wt", "ohi", c0, c1), A("m8", c0, c1), Alu.mult)
+            conv2(c0, c1, 4)
+        cp(A("m16"), IND("t16", "vlo"), "s")
+        ts(blk("ti", 3), blk("ti", 2), 4, Alu.arith_shift_right)
+        if rnd == 1:
+            tt(Z(0), blk("dha", 0), blk("dha", 1), Alu.add)
+        cp(A("vhi"), blk("ti", 3))
+        if rnd == 1:
+            tt(blk("af", 2), Z(0), blk("ida", 0), Alu.add)
+        tt(A("eqp"), P(4, 0, 64), blk("ida", 1), Alu.is_equal)
+        cp(A("nwp"), P(4, 64, 128))
+        tt(blk("thl", 0), IND("eqp", "pjo", 0, 64), blk("dha", 0), Alu.mult)
+        tt(blk("thl", 1), IND("eqp", "pjo", 0, 64), blk("dha", 1), Alu.mult)
+        table16(0, [blk("thl", 0), blk("thl", 1)], range(4))
+        table16(1, [blk("thl", 0), blk("thl", 1)], range(4, 8))
+        cp(A("dtab", 0, 256), P(0, 0, 256), "s")
+        tt(S1(1), IND("nwp", "pjo", 0, 64), blk("af", 1), Alu.subtract)
+        tt(S1(2), IND("eqp", "pjo", 0, 64), S1(1), Alu.mult)
+        tt(blk("af", 1), S1(2), blk("af", 1), Alu.add)
+        cp(A("on"), blk("af", 1))
+        cp(A("dtab", 256, 512), P(1, 256, 512))
+        if rnd == 1:
+            for t in (1, 0):
+                dma("y", D("do", None, t), blk("af", t + 1))
+            for t in (1, 0):
+                dma("y", D("lando", r, t), A("af", 64 * t + 64, 64 * t + 128, None, 16 * r, 16 * r + 16))
+            exchange("o")
+        for k in range(2):
+            cp(blk("gn", k, 512), IND(xt, "on", 512 * k, 512 * k + 512), "s")
+        mm(P(6), blk("idn", 1, 128), blk("xa", 0, 512), True, False)
+        mm(P(6), blk("idn", 0, 128), blk("gn", 0, 512), False, True)
+        for c0, c1 in CH:
+            tt(A("gp", c0, c1), IND("dtab", "vhi", c0, c1), A("m16", c0, c1), Alu.mult)
+            conv("gp", 0, c0, c1, ONES, 2)
+        act(blk("uu", 0, 512), P(6), Act.Identity, 4098.5)
+        mm(P(7), blk("idn", 1, 128), blk("xa", 1, 512), True, False)
+        mm(P(7), blk("idn", 0, 128), blk("gn", 1, 512), False, True)
+        act(blk("uu", 1, 512), P(7), Act.Identity, 4098.5)
+        if rnd == 0:
+            cp(blk("ah", 1), blk("af", 1))
+            tt(Z(0), blk("dha", 0), blk("dha", 1), Alu.add)
+            tt(blk("al", 1), blk("af", 1), blk("ah", 1), Alu.subtract)
+            tt(blk("af", 2), Z(0), blk("ida", 0), Alu.add)
+            table16(3, [blk("ah", 1), blk("al", 1)])
+            cp(blk("ft", 1, 512), P(3), "s")
+        tt(blk("af", 0), P(2, 0, 64), blk("af", 0), Alu.add)
+        if rnd == 0:
+            cp(blk("ah", 0), blk("af", 0))
+            cp(A("ov"), blk("af", 0))
+            tt(blk("al", 0), blk("af", 0), blk("ah", 0), Alu.subtract)
+            link_table(0, 0, "s")
+            link_table(1, 1, "s")
+        else:
+            cp(A("ov"), blk("af", 0))
+            dma("y", D("dv"), blk("af", 0))
+            dma("y", D("landv", r), A("af", 0, 64, None, 16 * r, 16 * r + 16))
+            exchange("v")
+        for hh, (c0, c1) in enumerate(HV):
+            tt(A("v16", c0, c1), IND(xt, "ov", c0, c1), A("uu", c0, c1), Alu.add)
+            ts(A("xa", c0, c1), A("v16", c0, c1), 0.25, Alu.mult, -1025.0, Alu.add)
+            if rnd == 1:
+                dma("y", D("dx%d" % hh), A("xa", c0, c1))
+                dma("s", D("landx%d" % hh, r), A("xa", c0, c1, None, 16 * r, 16 * r + 16))
+        if rnd == 0:
+            jobs = [(q, 0) for q in range(8)] + [(q, 1) for q in range(8)]
+            ring = [2, 3, 4, 6, 7, 1]
+
+            def rebuild(k0, k1, es):
+                for k in range(k0, k1):
+                    q, hh = jobs[k]
+                    e = es[(k - k0) % len(es)]
+                    if e != "V":
+                        mm(P(ring[k % 6]), blk("rep", q, 128), blk("xa", hh, 512), True, True)
+                    if e != "-":
+                        cp(blk("xt1", 2 * q + hh, 512), P(ring[k % 6]), e.lower())
+
+            cp(A("op"), blk("af", 2))
+            rebuild(0, 9, "vsssss--s")
+            for k in range(3):
+                link_chunk(k, 0)
+            rebuild(6, 8, "V")
+            rebuild(9, 11, "s")
+            link_lists(0)
+            cp(A("oab"), IND("abp", "pjo", 0, 128))
+            rebuild(11, 16, "vs")
+            table16(1, [blk("ah", 0), blk("al", 0)])
+            cp(blk("ft", 0, 512), P(1), "s")
+            cp(A("bfl", 0, 128), IND("ft", "flo", 0, 128, 1024), "s")
+
+    exchange("x0")
+    exchange("x1")
+    dma("y", X(T.yn[:]), D("lando", None, 0))
+    dma("s", X(T.yp[:]), D("lando", None, 1))
+    dma("y", X(T.yv[:]), D("landv"))
+    for hh, (c0, c1) in enumerate(HV):
+        dma("g", X(T.yx[:, c0:c1]), D("landx%d" % hh))
+
+    def meet(a, b):
+        return a[0] == b[0] and a[1] < b[2] and b[1] < a[2] and a[3] < b[4] and b[3] < a[4]
+
+    clock = {q: {} for q in Q}
+    seen = {}
+    for i, o in enumerate(ops):
+        o["waits"], o["sig"] = [], o["kind"] != "c"
+        o["lane"] = o["q"] if o["kind"] == "c" else o["sem"]
+        if o["kind"] != "a":
+            need = {}
+            for k, wr in [(k, True) for k in o["w"]] + [(k, False) for k in o["r"]]:
+                for j, kk, ww in seen.get(k[0], []):
+                    e = ops[j]
+                    if e["q"] == "p" and o["q"] == "p":
+                        continue
+                    bank = k[0].startswith("ps") and e["q"] != o["q"]
+                    if bank or ((wr or ww) and meet(k, kk)):
+                        need[e["lane"]] = max(need.get(e["lane"], -1), j)
+            ck = clock[o["q"]]
+            for j in sorted(need.values(), reverse=True):
+                e = ops[j]
+                if ck.get(e["lane"], -1) < j:
+                    o["waits"].append(j)
+                    e["sig"] = True
+                    for ln, v in e["clk"].items():
+                        if ck.get(ln, -1) < v:
+                            ck[ln] = v
+            o["clk"] = dict(ck)
+        else:
+            o["clk"] = {}
+        o["clk"][o["lane"]] = i
+        for k in o["w"]:
+            seen.setdefault(k[0], []).append((i, k, True))
+        for k in o["r"]:
+            seen.setdefault(k[0], []).append((i, k, False))
+    count, waited = {}, {}
+    for o in ops:
+        if o["kind"] == "c":
+            o["sem"], o["n"] = "c" + o["q"], 1
+        if o["sig"]:
+            count[o["sem"]] = count.get(o["sem"], 0) + o["n"]
+            o["at"] = count[o["sem"]]
+    for o in ops:
+        if o["kind"] == "a":
+            continue
+        for j in o["waits"]:
+            e = ops[j]
+            Q[o["q"]].wait_ge(T.sem[e["sem"]], e["at"])
+            waited[e["sem"]] = max(waited.get(e["sem"], 0), e["at"])
+        ins = o["fn"]()
+        if o["sig"] and o["kind"] != "r":
+            ins.then_inc(T.sem[o["sem"]], o["n"])
+    for sem in count:
+        if waited.get(sem, 0) < count[sem]:
+            g.wait_ge(T.sem[sem], count[sem])

@@ -4,27 +4,36 @@ from concourse.mybir import AluOpType, ActivationFunctionType
 F, B, I, U, H = "float32", "bfloat16", "int32", "uint16", "float16"
 SCRATCH = {}
 for _d, _names in {
-    I: "xi:1024 pi:8 thi:4 thb:4 la:192 pb:64 ti:256",
-    B: "sx:1024 land:1024 xa:1024 gn:1024 xt0:8192 xt1:8192 df:3072 rep:1024 xrep:1024 gm:2304 idn:256 i128:128 i1:128 "
-       "i8:128 jj:144 ah:192 al:192 abh:128 abl:128 wh:64 wl:64 dhl:128 dha:128 thl:128",
-    F: "uu:1024 sq:3072 gp:1024 m8:1024 m16:1024 lt:1024 wt:1024 dtab:512 ft:1536 pu:16 pvv:8 i16:16 i16b:16 pf:8 cc:8 "
-       "fl0:12 fl1:8 pj0:8 ida0:128 ida:128 idb:64 sel:32 t8:8 t16:16 thf:4 af:192 bfl:192 abp:128 abb:128 ee:192 uv:128 "
-       "pen:192 s1:512 eqp:64 nwp:64 ww:64",
-    U: "flo:12 flp:8 pjo:8 op:64 oab:128 olo:64 ohi:64 vlo:64 vhi:64 on:64 ov:64",
-    H: "v16:1024",
+    I: "xi:1024 pi:16 thi:4 la:192 ti:128 tv:320",
+    B: "sb:1024 sx:1024 xc:1024 gn:1024 xt0:8192 xt1:8192 rep:1024 km:512 idn:1664 fb:128 prm:256 i128:128 i1:128 ip:256 kb:256 "
+       "ks:256 thl:128 abh:128 abl:128 ah:192 al:192 ee:320 so:1024 back:1024",
+    F: "df:3072 sq:3072 uu:1024 gp:1024 m8:1024 m16:1024 lt:1024 wt:1024 dtab:512 ft:1536 xo:1024 repf:1024 pu:8 i16:16 pf:16 "
+       "cc:8 kc:4 f0:48 idc0:64 idc:64 idd:64 sel:40 i16b:16 t8:8 t16:16 thf:4 lc:128 ld:128 c0:192 c1:192 c2:192 abd:128 s1:512 lo:192",
+    U: "fac:24 fcd:12 fda:4 op:64 oab:128 olo:64 ohi:64 vlo:64 vhi:64 on:64 ov:64",
+    H: "v16:1024 w16:1024 fh:64",
 }.items():
     for _w in _names.split():
         SCRATCH[_w.split(":")[0]] = ("sbuf", [128, int(_w.split(":")[1])], _d)
-for _n, _w, _d in [("l", 16, I), ("p", 8, I), ("o", 16, F), ("v", 8, F), ("x0", 64, B), ("x1", 64, B)]:
-    SCRATCH["d" + _n] = ("dram", [8, 128, _w], _d)
+for _n, _w, _d in [("l", 16, I), ("p", 8, I), ("o", 16, F), ("v", 8, F)]:
+    SCRATCH["d" + _n + "s"] = ("dram", [8, 128, _w], _d)
     SCRATCH["land" + _n] = ("dram", [8, 128, _w], _d)
-for _k in range(8):
-    SCRATCH["ps%d" % _k] = ("psum", [128, 512], F)
-SEMAPHORES = (["cv", "cs", "cp", "cg"] + ["d%d" % k for k in range(60)] + ["arl", "arp", "aro", "arv", "arx0", "arx1", "arm"]
-              + ["ar%d" % k for k in range(1, 4)] + ["sn%d" % k for k in range(10)])
+for _k in range(4):
+    SCRATCH["pq%d" % _k] = ("psum", [128, 1024], F)
+SEMAPHORES = (["cv", "cs", "cp", "cg"] + ["d%d" % k for k in range(60)] + ["arl", "arp", "aro", "arv", "arm", "brm"]
+              + ["ar%d" % k for k in range(1, 4)] + ["br%d" % k for k in range(1, 4)] + ["sn%d" % k for k in range(14)])
 
+START, GATHER, WAKE, LOOKS, SLACK = {"v": 45, "s": 160}, 1.5, 110, [120, 60, 200, 90, 150], 2000
+LOCAL, REMOTE, WIRE, CALL, FIRST = 2300, 2600, 1300, 360, 2800
+WHOLE = [[0] * 4, [0] * 8]
+SHARE = [384, 384]
+SMALL, ABD, BOOSTS, GATE, TAIL, LATER = "v", "a", 0, 3, 7, 1200
+EARLY = 0.0002
+SWEEPS, SPREAD = 6, [(70, {}), (120, {"v": 15, "s": -20})]
+PAT, JOIN = 0, 0
+ON = ["aa", "vv", "vvv"]
+CA = [(0, 512), (512, 1024)]
+CB = [(0, 640), (640, 1024)]
 CH = [(0, 512), (512, 768), (768, 1024)]
-HV = [(0, 512), (512, 1024)]
 
 
 def rank_program(g, core, T, topo):
@@ -41,26 +50,27 @@ def rank_program(g, core, T, topo):
         if c0 is None:
             c0, c1 = 0, t.shape[1]
         ap = t[p0:p1, c0:c1:st] if st else t[p0:p1, c0:c1]
-        return ap, [(name, p0, p1, c0, c1)]
+        return ap, [(name, p0, p1, c0, c1, st or 1)], len(range(c0, c1, st or 1)), SCRATCH[name]
 
     def D(name, k=None, t=None):
         b = T[name]
         if t is None:
             ap = b[:] if k is None else b[k]
         else:
-            ap = b[:, 64 * t:64 * t + 64, :] if k is None else b[k, 64 * t:64 * t + 64, :]
-        return ap, [(name, 0 if k is None else k, 8 if k is None else k + 1, 0 if t is None else t, 4 if t is None else t + 1)]
+            n = 1024 // b.shape[2]
+            ap = b[:, n * t:n * t + n, :] if k is None else b[k, n * t:n * t + n, :]
+        return ap, [(name, 0 if k is None else k, 8 if k is None else k + 1, 0 if t is None else t, 4 if t is None else t + 1, 1)]
 
     def X(ap):
         return ap, []
 
-    def IND(win, off, c0=0, c1=1024, w1=None):
-        w, o = (A(win) if w1 is None else A(win, 0, w1)), A(off, c0 // 16, c1 // 16)
-        return w[0].indirect(o[0]), w[1] + o[1]
+    def IND(win, off, c0=0, c1=1024, w0=None, w1=None):
+        w, o = A(win, w0, w1), A(off, c0 // 16, c1 // 16)
+        return w[0].indirect(o[0]), w[1] + o[1], c1 - c0, None
 
-    def add(q, fn, outs, ins, kind="c", sem=None, n=0):
+    def add(q, fn, outs, ins, hold, kind="c", sem=None, n=0, flight=0):
         ops.append({"q": q, "fn": fn, "w": [k for o in outs for k in o[1]], "r": [k for o in ins for k in o[1]],
-                    "kind": kind, "sem": sem, "n": n})
+                    "kind": kind, "sem": sem, "n": n, "hold": hold, "flight": flight})
 
     def col(s):
         return [s] if isinstance(s, tuple) else []
@@ -68,46 +78,59 @@ def rank_program(g, core, T, topo):
     def val(s):
         return s[0] if isinstance(s, tuple) else s
 
+    def cycles(q, a, rate):
+        return 70 + GATHER * a[2] if a[3] is None else max(64, START[q] + rate * a[2])
+
+    def short(*xs):
+        return 0.5 if all(x[3] and x[3][2] in (B, H, U) for x in xs) else 1
+
     def tt(o, a, b, op):
-        add("v", lambda: g.vector.tensor_tensor(o[0], a[0], b[0], op), [o], [a, b])
+        add("v", lambda: g.vector.tensor_tensor(o[0], a[0], b[0], op), [o], [a, b],
+            cycles("v", a, 2 if a[3] and a[3][0] == b[3][0] else 1))
 
     def ts(o, a, s1, op0, s2=None, op1=None):
         if op1 is None:
-            add("v", lambda: g.vector.tensor_scalar(o[0], a[0], val(s1), None, op0), [o], [a] + col(s1))
+            add("v", lambda: g.vector.tensor_scalar(o[0], a[0], val(s1), None, op0), [o], [a] + col(s1), cycles("v", a, short(o, a)))
         else:
-            add("v", lambda: g.vector.tensor_scalar(o[0], a[0], val(s1), val(s2), op0, op1), [o], [a] + col(s1) + col(s2))
+            add("v", lambda: g.vector.tensor_scalar(o[0], a[0], val(s1), val(s2), op0, op1), [o], [a] + col(s1) + col(s2),
+                cycles("v", a, short(o, a)))
 
-    def cp(o, a, q="v"):
-        if q == "v":
-            add("v", lambda: g.vector.tensor_copy(o[0], a[0]), [o], [a])
-        else:
-            add("s", lambda: g.scalar.activation(o[0], a[0], Act.Copy), [o], [a])
+    def chain(o, a, b):
+        add("v", lambda: g.vector.tensor_tensor_scan(o[0], a[0], b[0], 0.0, Alu.mult, Alu.add), [o], [a, b], cycles("v", a, 1))
 
     def act(o, a, f, bias=0.0, scale=1.0):
-        add("s", lambda: g.scalar.activation(o[0], a[0], f, bias=bias, scale=scale), [o], [a])
+        add("s", lambda: g.scalar.activation(o[0], a[0], f, bias=bias, scale=scale), [o], [a], cycles("s", a, 1))
 
-    def mm(o, l, m, st, sp):
-        add("p", lambda: g.tensor.matmul(o[0], l[0], m[0], st, sp), [o], [l, m])
-
-    def iota(o, pat, base, cm, flt=True):
-        if flt:
-            add("g", lambda: g.iota(o[0], pat, base, cm, allow_small_or_imprecise_dtypes=True), [o], [])
+    def cp(o, a, q="v", bias=None):
+        if bias is None:
+            fns = {"v": lambda: g.vector.tensor_copy(o[0], a[0]), "s": lambda: g.scalar.activation(o[0], a[0], Act.Copy)}
         else:
-            add("g", lambda: g.iota(o[0], pat, base, cm), [o], [])
+            fns = {"v": lambda: g.vector.tensor_scalar(o[0], a[0], bias, None, Alu.add),
+                   "s": lambda: g.scalar.activation(o[0], a[0], Act.Identity, bias=bias)}
+        add(q, fns, [o], [a], {"v": cycles("v", a, short(o, a)), "s": cycles("s", a, 1)})
+
+    def mm(o, l, m, st=True, sp=True):
+        add("p", lambda: g.tensor.matmul(o[0], l[0], m[0], st, sp), [o], [l, m], max(64, m[2]) * (2.4 if m[3][2] == F else 0.6))
+
+    def iota(o, pat, base, cm, flt=True, after=()):
+        if flt:
+            add("g", lambda: g.iota(o[0], pat, base, cm, allow_small_or_imprecise_dtypes=True), [o], list(after), 160 + 2 * o[2])
+        else:
+            add("g", lambda: g.iota(o[0], pat, base, cm), [o], [], 160 + 2 * o[2])
 
     nd = [0]
 
-    def dma(q, o, a):
+    def dma(q, o, a, more=0):
         sem = "d%d" % nd[0]
         nd[0] += 1
-        add(q, lambda: Q[q].dma_start(o[0], a[0]), [o], [a], "d", sem, 16)
+        add(q, lambda: Q[q].dma_start(o[0], a[0]), [o], [a], 60, "d", sem, 16, LOCAL + more)
 
-    ns = [0]
+    ns, sent = [0], {}
 
     def bits(es):
         return sum(1 << e for e in es)
 
-    def send(items):
+    def send(items, after=()):
         sem = "sn%d" % ns[0]
         ns[0] += 1
         trs = []
@@ -115,18 +138,23 @@ def rank_program(g, core, T, topo):
             rid, pid, _ = topo.addr(cores[q])
             trs.append(RemoteDMATransfer(dst_ids=[DstId(rid=rid, pnc=pid)], dma_engine_mask=bits(es),
                                          remote_sem=T.sem[rs], src=src[0], dst=dst))
-        add("g", lambda: g.remote_dma_fused(trs, local_sem=T.sem[sem]), [], [i[2] for i in items], "r", sem,
-            sum(len(i[1]) for i in items))
+        add("g", lambda: g.remote_dma_fused(trs, local_sem=T.sem[sem]), [], [i[2] for i in items] + list(after),
+            FIRST if ns[0] == 1 else CALL, "r", sem, sum(len(i[1]) for i in items), REMOTE)
+        if len(items) > 1:
+            ops[-1]["wire"] = WIRE if SCRATCH[items[0][2][1][0][0]][0] == "sbuf" else WIRE // 3
+        for i in items:
+            sent[i[4]] = len(ops) - 1
 
     def arrive(outs, sem, n):
-        add(None, None, outs, [], "a", sem, n)
+        add(None, None, outs, [], 0, "a", sem, n)
+        ops[-1]["like"] = sent[sem]
 
     chips = sorted(set(topo.chip(c) for c in cores))
     on = [[q for q in range(8) if topo.chip(cores[q]) == ch] for ch in chips]
     ci = chips.index(topo.chip(core))
     mate = [q for q in on[ci] if q != r][0]
-    to = [None] + [on[(ci + k) % 4] for k in (1, 2, 3)]
-    fr = [None] + [on[(ci - k) % 4] for k in (1, 2, 3)]
+    to = [on[(ci + k) % 4] for k in range(4)]
+    fr = [on[(ci - k) % 4] for k in range(4)]
     far = topo.engines(core, cores[to[1][0]])
     near = [e for e in topo.engines(core, cores[mate]) if e not in far]
     hf = len(far) // 2
@@ -134,13 +162,15 @@ def rank_program(g, core, T, topo):
     solo = far[0::2] + far[1::2]
 
     def exchange(n):
-        src, dst, sem = "d" + n, "land" + n, "ar" + n
+        src, dst, sem = "d" + n + "s", "land" + n, "ar" + n
         send([(mate, near[:2], D(src, mate), T[dst][r], sem)]
              + [(q, [solo[j]], D(src, q), T[dst][r], sem) for j, q in enumerate(others)])
         arrive([D(dst, q) for q in range(8) if q != r], sem, 8)
 
-    def P(k, c0=None, c1=None, st=None):
-        return A("ps%d" % k, c0, c1, st)
+    def P(k, c0=0, c1=512, st=1):
+        b0 = 512 * (k % 2)
+        return (T["pq%d" % (k // 2)][:, b0 + c0:b0 + c1:st], [("ps%d" % (k + j), 0, 128, c0, c1, st) for j in range(1 + (c1 > 512))],
+                len(range(c0, c1, st)), SCRATCH["pq0"])
 
     def blk(name, k, n=64):
         return A(name, n * k, n * k + n)
@@ -149,63 +179,20 @@ def rank_program(g, core, T, topo):
         return blk("s1", k)
 
     def Z(k):
-        return blk("ps5", k)
+        return P(5, 64 * k, 64 * k + 64)
+
+    SHR, AND = Alu.arith_shift_right, Alu.bitwise_and
 
     lists = [T.prv, T.nxt, T.ptn]
     for t in range(3):
-        dma("y" if t % 2 == 0 else "s", D("dl", None, t) if t < 2 else D("dp"), X(lists[t][:]))
+        dma("y" if t % 2 == 0 else "s", D("dls", None, t) if t < 2 else D("dps"), X(lists[t][:]))
     order = to[1] + [mate] + to[2] + to[3] + [r]
     for j, q in enumerate(order):
-        dma("s" if j % 2 == 0 else "y", blk("xi", j, 128), X(T.x[16 * q:16 * q + 16, :]))
+        dma("s" if j % 2 == 0 else "y", blk("xi", j, 128), X(T.x[16 * q:16 * q + 16, :]), 700 + 350 * j)
     for t in range(3):
         dma("s", D("landl", r, t) if t < 2 else D("landp", r), X(lists[t][16 * r:16 * r + 16, :]))
-
-    iota(A("i8"), [[0, 8], [8, 16]], 0, 0)
-    iota(A("pvv"), [[-1, 8]], 0, 1)
-    iota(A("pi", 0, 1), [[0, 1]], 0, 1, False)
-    iota(A("i1"), [[0, 8], [1, 16]], 0, 0)
-    iota(A("pu"), [[-8, 16]], 0, 1)
-    iota(A("jj"), [[0, 9], [200, 2], [1, 8]], -200, 0)
-    exchange("l")
     for k in range(8):
-        ts(blk("xrep", k, 128), A("i8"), A("pvv", k, k + 1), Alu.is_equal)
-    for k, (s1, o0) in enumerate([(7, Alu.bitwise_and), (15, Alu.bitwise_and), (3, Alu.arith_shift_right), (4, Alu.arith_shift_right)]):
-        ts(A("pi", k + 1, k + 2), A("pi", 0, 1), s1, o0)
-    ts(A("pi", 5, 6), A("pi", 0, 1), 3, Alu.arith_shift_right, 1, Alu.bitwise_and)
-    for k in range(8):
-        ts(blk("rep", k, 128), A("i1"), A("pu", 2 * k, 2 * k + 1), Alu.is_equal)
-    cp(A("pf", 0, 6), A("pi", 0, 6))
-
-    def piece(j):
-        return blk("sx", j, 128)
-
-    mine = T.land[:, 128 * r:128 * r + 128]
-    cp(A("sx", 0, 384), A("xi", 0, 384))
-    send([(to[1][0], far[:hf], piece(0), mine, "ar1"), (to[1][1], far[hf:], piece(1), mine, "ar1"),
-          (mate, near, piece(2), mine, "arm")])
-    exchange("p")
-    cp(A("sx", 384, 640), A("xi", 384, 640))
-    send([(to[2][0], far[:hf], piece(3), mine, "ar2"), (to[2][1], far[hf:], piece(4), mine, "ar2")])
-    cp(A("sx", 640, 896), A("xi", 640, 896))
-    send([(to[3][0], far[:hf], piece(5), mine, "ar3"), (to[3][1], far[hf:], piece(6), mine, "ar3")])
-    cp(blk("land", r, 128), A("xi", 896, 1024))
-    arrive([blk("land", mate, 128)], "arm", len(near))
-    for k in (1, 2, 3):
-        arrive([blk("land", q, 128) for q in fr[k]], "ar%d" % k, 2 * hf)
-
-    iota(A("i16b"), [[1, 2], [2, 8]], 0, 0)
-    iota(A("i16"), [[1, 16]], 0, 0)
-    iota(A("fl0"), [[512, 3], [16, 4]], 0, 0)
-    iota(A("fl1"), [[512, 2], [2, 4]], 0, 0)
-    iota(A("pj0"), [[64, 2], [2, 4]], 0, 0)
-    iota(A("idb"), [[128, 8], [1024, 8]], 0, 1)
-    iota(A("ida0", 0, 64), [[16, 64]], 0, 1)
-    iota(A("ida0", 64, 128), [[16, 8], [128, 8]], 0, 1)
-    iota(A("i128"), [[1, 128]], 0, 0)
-    dma("g", A("thi", 0, 1, None, 0, 2), X(T.th[16 * r:16 * r + 2, :]))
-    add("g", lambda: g.partition_broadcast(T.thb[:, 0:1], T.thi[0:1, 0:1], 128), [A("thb")], [A("thi")])
-    for k in range(16):
-        ts(blk("gm", k, 144), A("jj"), A("pu", k, k + 1), Alu.is_equal)
+        dma("y", A("thi", 0, 1, None, 16 * k, 16 * k + 16), X(T.th[16 * r:16 * r + 16, :]), 9000)
 
     def pf(k):
         return A("pf", k, k + 1)
@@ -213,286 +200,522 @@ def rank_program(g, core, T, topo):
     def cc(k):
         return A("cc", k, k + 1)
 
-    def constants():
-        ts(cc(0), pf(1), 64.0, Alu.mult, pf(4), Alu.add)
-        ts(cc(2), pf(1), 8.0, Alu.mult, pf(5), Alu.add)
-        ts(cc(3), pf(4), 1008.0, Alu.mult)
-        ts(cc(6), pf(4), 8.0, Alu.mult, pf(5), Alu.add)
-        ts(A("sel", 0, 16), A("i16b"), pf(3), Alu.is_equal)
-        ts(cc(1), pf(5), 8.0, Alu.mult, cc(0), Alu.add)
-        ts(cc(7), pf(1), 64.0, Alu.mult, cc(6), Alu.add)
-        ts(A("t8"), A("i16", 0, 8), pf(1), Alu.is_equal)
-        ts(A("t16"), A("i16"), pf(2), Alu.is_equal)
-        tt(A("sel", 16, 24), A("sel", 0, 8), A("sel", 8, 16), Alu.add)
-        ts(A("flp"), A("fl1"), cc(7), Alu.add)
-        ts(A("pjo"), A("pj0"), cc(2), Alu.add)
-        ts(A("ida"), A("ida0"), cc(3), Alu.add)
-        ts(A("flo"), A("fl0"), cc(1), Alu.add)
-        ts(A("sel", 24, 32), A("sel", 16, 24), 2.0 ** -21, Alu.mult)
-        for k, v in enumerate([1.0, 2.0]):
-            ts(blk("idn", k, 128), A("i128"), pf(0), Alu.is_equal, v, Alu.mult)
+    iota(A("pu"), [[-16, 8]], 0, 1)
+    iota(A("ip", 0, 128), [[1, 8], [8, 16]], 0, 0)
+    iota(A("i1"), [[0, 8], [1, 16]], 0, 0)
+    iota(A("pi", 0, 1), [[0, 1]], 0, 1, False)
+    iota(A("i128"), [[1, 128]], 0, 0)
+    iota(A("i16"), [[1, 16]], 0, 0)
+    exchange("l")
+    if PAT == 0:
+        exchange("p")
+    ts(blk("prm", 0, 128), blk("ip", 0, 128), A("pu", 0, 1), Alu.is_equal)
 
-    ONES, DIST = A("sel", 16, 24), A("sel", 24, 32)
+    def pieces(src, j, qs, dst, sem):
+        return [(qs[0], far[:hf], blk(src, j, 128), dst, sem), (qs[1], far[hf:], blk(src, j + 1, 128), dst, sem)]
 
-    def conv(src, base, c0, c1, sel, bank, c=0):
+    def turn(j0, j1, bank, out):
+        cp(A("sb", 128 * j0, 128 * j1), A("xi", 128 * j0, 128 * j1))
+        mm(P(bank, 0, 128 * (j1 - j0)), blk("prm", 0, 128), A("sb", 128 * j0, 128 * j1))
+        cp(out, P(bank, 0, 128 * (j1 - j0)), "s")
+
+    mine = T.xc[:, 128 * r:128 * r + 128]
+    turn(0, 3, 0, A("sx", 0, 384))
+    send(pieces("sx", 0, to[1], mine, "ar1") + [(mate, near, blk("sx", 2, 128), mine, "arm")])
+    if PAT == 1:
+        exchange("p")
+    turn(3, 5, 1, A("sx", 384, 640))
+    if GATE == 3:
+        send(pieces("sx", 3, to[2], mine, "ar2"))
+    turn(5, 7, 6, A("sx", 640, 896))
+    turn(7, 8, 7, blk("xc", r, 128))
+    iota(A("f0", 0, 12), [[512, 3], [128, 4]], 0, 0)
+    iota(A("f0", 12, 24), [[-512, 3], [16, 4]], 1024, 0)
+    iota(A("f0", 24, 28), [[2, 4]], 1024, 0)
+    iota(A("idd"), [[1024, 8], [128, 8]], 0, 1)
+    iota(A("idc0"), [[1024, 8], [16, 8]], 0, 1)
+    iota(A("ip", 128, 256), [[1, 16], [16, 8]], 0, 0, True, [D("landl"), D("landp")])
+    ops[-1]["flight"] = 20000
+    if GATE == 2:
+        send(pieces("sx", 3, to[2], mine, "ar2"))
+    send(pieces("sx", 5, to[3], mine, "ar3"))
+    iota(A("c1"), [[0, 64], [1, 3]], 0, 0)
+    ops[-1]["flight"] = 6000
+    arrive([blk("xc", mate, 128)], "arm", len(near))
+    for k in (1, 2, 3):
+        arrive([blk("xc", q, 128) for q in fr[k]], "ar%d" % k, 2 * hf)
+        ops[-1]["flight"] = LATER if k == 2 else 0
+
+    for k in range(8):
+        ts(blk("rep", k, 128), A("i1"), A("pu", k, k + 1), Alu.is_equal)
+    for k, (sh, m) in enumerate([(0, 7), (0, 15), (3, 15), (4, 7), (3, 1), (5, 1), (2, 7), (0, 3)]):
+        ts(A("pi", k + 1, k + 2), A("pi", 0, 1), sh, SHR, m, AND)
+    cp(A("pf", 0, 9), A("pi", 0, 9))
+    cp(A("repf"), A("rep"), "s")
+    ts(cc(6), pf(6), 8.0, Alu.mult, pf(7), Alu.add)
+    ts(A("kc"), A("i16", 0, 4), pf(8), Alu.not_equal, 100.0, Alu.mult)
+    for k, v in enumerate([1.0, 2.0, 2.0 ** 21, 2.0 ** 23, -1.0, 1 / 16, 7 / 16, -63 / 128]):
+        ts(blk("idn", k, 128), A("i128"), pf(0), Alu.is_equal, v, Alu.mult)
+    ts(A("kc"), A("kc"), cc(6), Alu.add)
+    ts(cc(0), pf(5), 64.0, Alu.mult, pf(1), Alu.add)
+    ts(cc(2), pf(5), 64.0, Alu.mult, pf(4), Alu.add)
+    ts(cc(3), pf(1), 64.0, Alu.mult, pf(4), Alu.add)
+    ts(cc(4), pf(1), 64.0, Alu.mult, pf(5), Alu.add)
+    for j in range(4):
+        ts(blk("km", j, 128), A("i1"), A("kc", j, j + 1), Alu.is_equal)
+    ts(cc(0), pf(4), 8.0, Alu.mult, cc(0), Alu.add)
+    ts(cc(2), pf(1), 8.0, Alu.mult, cc(2), Alu.add)
+    ts(cc(3), pf(5), 8.0, Alu.mult, cc(3), Alu.add)
+    ts(cc(4), pf(4), 8.0, Alu.mult, cc(4), Alu.add)
+    ts(cc(5), pf(4), 112.0, Alu.mult)
+    ts(A("t8"), A("i16", 0, 8), pf(1), Alu.is_equal)
+    ts(A("t16"), A("i16"), pf(2), Alu.is_equal)
+    ts(A("sel", 0, 16), A("i16"), pf(3), Alu.is_equal)
+    ts(A("sel", 16, 24), A("i16", 0, 8), pf(4), Alu.is_equal)
+    ts(A("fac", 0, 12), A("f0", 0, 12), cc(0), Alu.add)
+    ts(A("fac", 12, 24), A("f0", 0, 12), cc(2), Alu.add)
+    ts(A("fcd"), A("f0", 12, 24), cc(3), Alu.add)
+    ts(A("fda"), A("f0", 24, 28), cc(4), Alu.add)
+    ts(A("idc"), A("idc0"), cc(5), Alu.add)
+
+    ts(A("c0"), A("c1"), 0.5, Alu.mult)
+
+    ONES, PD = A("sel", 16, 24), A("c2", 1, 192, 3)
+
+    def conv(src, base, c0, c1, bank, opened=False, last=False):
         for b in range(c0 // 128, c1 // 128):
-            mm(P(bank, c + 8 * b, c + 8 * b + 8), A(src, base + 128 * b, base + 128 * b + 128), sel, True, True)
+            mm(P(bank, 8 * b, 8 * b + 8), A(src, base + 128 * b, base + 128 * b + 128), ONES, not opened, not opened or (last and b == 7))
 
     def conv2(c0, c1, bank):
         for b in range(c0 // 128, c1 // 128):
-            mm(P(bank, b, 128, 8), A("gp", 128 * b, 128 * b + 128), A("sel", 0, 16), True, True)
+            mm(P(bank, 16 * b, 16 * b + 16), A("gp", 128 * b, 128 * b + 128), A("sel", 0, 16))
+
+    def two(name, k):
+        return P(name, k, 128, 2) if isinstance(name, int) else A(name, k, 128, 2)
 
     def table16(bank, pts, qs=range(8)):
         for q in qs:
             for j, pt in enumerate(pts):
-                mm(P(bank, 64 * q, 64 * q + 64), blk("rep", q, 128), pt, j == 0, j == len(pts) - 1)
+                mm(P(bank, 64 * q, 64 * q + 64), blk("repf" if pt[3][2] == F else "rep", q, 128), pt, j == 0, j == len(pts) - 1)
 
-    def gmat(u, t):
-        return A("gm", 144 * u + 8 - 8 * t, 144 * u + 136 - 8 * t)
+    def split(h, lo, src, q="v"):
+        cp(h, src, q)
+        tt(lo, src, h, Alu.subtract)
 
-    def link_table(s3, bank, e):
-        for q in range(8):
-            for j, (t, nm) in enumerate([(1, "ah"), (1, "al"), (0, "ah"), (0, "al")]):
-                mm(P(bank, 64 * q, 64 * q + 64), gmat(2 * q + s3, t), blk(nm, t), j == 0, j == 3)
-        cp(A("lt", s3, 1024, 2), P(bank), e)
+    def table8(out, bank, banks, q):
+        for e in range(2):
+            mm(P(bank, 128 * e, 128 * e + 128), A("kb", e, 256, 2), blk("idn", 0, 128))
+        cp(A("ks"), P(bank, 0, 256), q)
+        for hh, bk in enumerate(banks):
+            for j in range(2):
+                mm(P(bk, 256 * j, 256 * j + 256), blk("km", 2 * hh + j, 128), A("ks"))
+            cp(blk(out, hh, 512), P(bk), "a" if out == "lt" else ON[0][hh])
 
-    def flip_mm(banks, ptss):
-        for bk, pts in zip(banks, ptss):
-            table16(bk, pts)
-
-    def flip_out(banks, out):
-        for j, bk in enumerate(banks):
-            cp(blk("ft", j, 512), P(bk), "s")
-        n = len(banks)
-        cp(out, IND("ft", "flo", 0, 64 * n, 512 * n), "s")
-
-    def parts(h, lo, n):
-        return [[blk(h, t), blk(lo, t)] for t in range(n)]
-
-    def link_chunk(k, bank):
+    def masked(tab, off, mask, k):
         c0, c1 = CH[k]
-        tt(A("gp", c0, c1), IND("lt", "ohi", c0, c1), A("m8", c0, c1), Alu.mult)
-        conv2(c0, c1, bank)
+        tt(A("gp", c0, c1), IND(tab, off, c0, c1), A(mask, c0, c1), Alu.mult)
+        return c0, c1
 
-    def link_lists(bank):
-        cp(A("abh"), P(bank, 0, 128))
-        tt(A("abl"), P(bank, 0, 128), A("abh"), Alu.subtract)
-        cp(A("abp"), P(bank, 0, 128))
+    def partner_row():
+        ts(A("olo"), PD, 2.0 ** -10, Alu.mult, -0.49951171875, Alu.add)
+
+    def partner_column():
+        cp(blk("ti", 0), PD)
+        ts(blk("ti", 1), blk("ti", 0), 1023, AND)
+        cp(A("ohi"), blk("ti", 1))
+
+    def partner_links():
+        split(A("kb", 0, 128), A("kb", 128, 256), A("ld"))
+        table8("lt", 4, [0, 1], "v")
+        for k in range(3):
+            conv2(*masked("lt", "ohi", "m8", k), 4)
+
+    def partner_lists():
+        split(A("abh"), A("abl"), P(4, 0, 128), ON[2][1])
+        cp(blk("oab", 1), two(4, 1))
+        cp(blk("oab", 0), two(4, 0))
+        for t in (1, 0):
+            table16(6 + t, [two("abh", t), two("abl", t)])
 
     def closed():
-        tt(Z(0), A("pb"), A("idb"), Alu.is_equal)
-        tt(blk("ee", 1), A("pb"), blk("bfl", 1), Alu.is_equal)
-        tt(blk("ee", 2), A("pb"), blk("bfl", 0), Alu.is_equal)
-        tt(Z(2), Z(0), blk("ee", 1), Alu.max)
-        tt(Z(3), Z(0), blk("ee", 2), Alu.max)
-        cp(blk("ti", 2), blk("bfl", 0))
-        tt(blk("pen", 0), Z(3), blk("ee", 1), Alu.max)
-        ts(blk("ti", 0), blk("ti", 2), 15, Alu.bitwise_and)
-        tt(blk("uv", 0), blk("abb", 0), blk("bfl", 1), Alu.is_equal)
-        cp(A("vlo"), blk("ti", 0))
-        tt(blk("uv", 1), blk("abb", 1), blk("bfl", 0), Alu.is_equal)
-        tt(S1(0), blk("abb", 1), A("pb"), Alu.subtract)
-        tt(A("pen", 64, 192), A("ps5", 128, 256), A("uv"), Alu.max)
+        tt(blk("ee", 0), PD, A("idd"), Alu.is_equal)
+        tt(blk("ee", 1), PD, blk("ld", 1), Alu.is_equal)
+        tt(blk("ee", 2), PD, blk("ld", 0), Alu.is_equal)
 
-    nb = [0]
+    def fields(n):
+        ts(A("fh"), n, 16400 - 7.5, Alu.add)
+        ts(blk("fb", 0), n, 132096 - 511.5, Alu.add)
+        ts(blk("fb", 1), n, 16512 - 63.5, Alu.add)
 
-    def points(qs, es):
-        for q in qs:
-            for hh in range(2):
-                bk = 2 + nb[0] % 3
-                for vh in range(4 * hh, 4 * hh + 4):
-                    mm(P(bk, 128 * (vh % 4), 128 * (vh % 4) + 128), blk("xrep", vh, 128), blk("land", q, 128), True, True)
-                cp(blk("xt0", 2 * q + hh, 512), P(bk), es[nb[0] % len(es)])
-                nb[0] += 1
+    def prv_place():
+        fields(blk("ld", 0))
+        for j, (w, x) in enumerate([(0, blk("kb", 0)), (0, blk("kb", 2)), (4, A("fh"))]):
+            mm(Z(6), blk("idn", w, 128), x, j == 0, j == 2)
+        for j, (w, x) in enumerate([(5, A("fh")), (6, blk("fb", 1)), (7, blk("fb", 0))]):
+            mm(Z(7), blk("idn", w, 128), x, j == 0, j == 2)
+        ts(A("vlo"), Z(6), 16400.0, Alu.add)
+        ts(A("vhi"), Z(7), 132096 * 63 / 128 - 16512 * 7 / 16 - 16400 / 16, Alu.add)
 
-    points([r], "s")
-    constants()
-    points([mate] + fr[1], "sv")
+    def points(xt, src, qs, pairs, whole, bias=None):
+        for q, bk, w in zip(qs, pairs, whole):
+            for b in range(8):
+                mm(P(bk + b // 4, 128 * (b % 4), 128 * (b % 4) + 128), blk("rep", b, 128), blk(src, q, 128))
+                if b == 7 and w:
+                    cp(blk(xt, q, 1024), P(bk, 0, 1024), "s", bias)
+                elif b % 4 == 3 and not w:
+                    cp(blk(xt, 2 * q + b // 4, 512), P(bk + b // 4), "a", bias)
+
+    points("xt0", "xc", [r], [2], [0])
     for t in range(3):
         dma("y", blk("la", t), D("landl", None, t) if t < 2 else D("landp"))
-    for q in [r, mate] + fr[1] + fr[2] + fr[3]:
-        dma("y", A("xa", 0, 1024, None, 16 * q, 16 * q + 16), blk("land", q, 128))
-    points(fr[2][:1], "s")
-    cp(A("ah", 0, 128), A("la", 0, 128))
-    tt(A("al", 0, 128), A("la", 0, 128), A("ah", 0, 128), Alu.subtract)
-    ts(blk("ti", 0), blk("la", 2), 7, Alu.bitwise_and)
-    ts(blk("ti", 1), blk("la", 2), 3, Alu.arith_shift_right)
-    cp(A("olo"), blk("ti", 0))
-    points(fr[2][1:], "s")
-    cp(A("m8"), IND("t8", "olo"), "s")
-    cp(blk("ah", 2), blk("la", 2))
-    cp(A("op"), blk("la", 2))
-    tt(blk("al", 2), blk("la", 2), blk("ah", 2), Alu.subtract)
-    cp(A("ohi"), blk("ti", 1))
-    cp(A("af", 0, 128), A("la", 0, 128))
-    ts(A("thf", 0, 1), A("thb", 0, 1), 2.0 ** -21, Alu.mult)
-    link_table(0, 0, "v")
-    link_table(1, 1, "v")
-    points(fr[3], "s")
-    for k in range(3):
-        link_chunk(k, 0)
-    link_lists(0)
+    points("xt0", "xc", [mate] + fr[1], [6, 2, 6], [0, 0, 0])
+    split(A("ah", 0, 128), A("al", 0, 128), A("la", 0, 128))
+    split(blk("ah", 2), blk("al", 2), blk("la", 2))
+    for t, bk in [(0, 0), (1, 1), (2, 4)]:
+        table16(bk, [blk("ah", t), blk("al", t)])
+        cp(blk("ft", t, 512), P(bk), "a")
+    cp(A("ld"), IND("ft", "fac", 192, 320, 0, 1024), "a")
+    cp(PD, IND("ft", "fac", 320, 384))
+    partner_row()
+    for c0 in (0, 512):
+        cp(A("m8", c0, c0 + 512), IND("t8", "olo", c0, c0 + 512), "s")
+    partner_column()
+    partner_links()
+    cp(A("op"), IND("ft", "fac", 128, 192))
+    points("xt0", "xc", fr[2] + fr[3], [2, 6, 2, 0], WHOLE[0])
+    partner_lists()
+    cp(A("lc"), IND("ft", "fac", 0, 128, 0, 1024), "a")
+    closed()
+    prv_place()
+    ts(blk("prm", 1, 128), blk("ip", 1, 128), pf(0), Alu.is_equal, 0.0625, Alu.mult)
+    cp(A("thf", 0, 1), A("thi", 0, 1))
 
     for rnd in range(2):
-        xt = "xt%d" % rnd
-        flip_mm([3, 2], parts("abh", "abl", 2)[::-1])
-        cp(blk("ft", 1, 512), P(3), "s")
-        cp(blk("ft", 0, 512), P(2), "s")
-        tt(A("df", 0, 1024), IND(xt, "op"), A("xa"), Alu.subtract)
-        if rnd == 0:
-            cp(A("oab"), IND("ft", "flp", 0, 128, 1024))
-            cp(A("abb"), IND("abp", "pjo", 0, 128), "s")
-            flip_mm([6, 7, 2], parts("ah", "al", 3))
-            flip_out([6, 7, 2], A("bfl"))
-        else:
-            cp(A("abb"), IND("ft", "flp", 0, 128, 1024), "s")
-        tt(A("df", 1024, 2048), IND(xt, "oab", 1024, 2048), A("xa"), Alu.subtract)
-        act(A("sq", 0, 1024), A("df", 0, 1024), Act.Square)
-        conv("sq", 0, 0, 1024, DIST, 0)
-        act(A("sq", 1024, 2048), A("df", 1024, 2048), Act.Square)
-        conv("sq", 1024, 0, 1024, DIST, 0, 64)
-        for c0, c1 in CH:
-            tt(A("df", 2048 + c0, 2048 + c1), IND(xt, "oab", c0, c1), A("xa", c0, c1), Alu.subtract)
-            if c0 == 0:
-                if rnd == 0:
-                    cp(A("pb"), blk("bfl", 2))
-                closed()
-            act(A("sq", 2048 + c0, 2048 + c1), A("df", 2048 + c0, 2048 + c1), Act.Square)
-            conv("sq", 2048, c0, c1, DIST, 1)
-        tt(S1(1), P(0, 0, 64), blk("pen", 0), Alu.max)
-        tt(Z(0), P(0, 64, 128), blk("pen", 2), Alu.max)
-        tt(Z(1), Z(0), S1(1), Alu.is_lt)
-        tt(S1(2), Z(0), S1(1), Alu.min)
-        tt(Z(2), Z(1), S1(0), Alu.mult)
-        tt(Z(3), Z(2), A("pb"), Alu.add)
-        tt(Z(4), P(1, 0, 64), blk("pen", 1), Alu.max)
-        tt(S1(5), Z(3), blk("abb", 0), Alu.subtract)
-        tt(Z(5), Z(4), S1(2), Alu.is_lt)
-        cp(S1(4), Z(3))
-        tt(S1(7), Z(4), S1(2), Alu.min)
-        tt(Z(6), Z(5), S1(5), Alu.mult)
-        ts(Z(7), S1(7), A("thf", 0, 1), Alu.is_ge, 8192.0, Alu.mult)
-        tt(A("pb"), S1(4), Z(6), Alu.subtract)
-        tt(Z(0), Z(7), blk("bfl", 0), Alu.subtract)
-        ts(blk("ti", 0), A("pb"), 7, Alu.bitwise_and)
-        tt(A("ww"), Z(0), A("pb"), Alu.add)
-        cp(A("olo"), blk("ti", 0))
-        cp(A("wh"), IND("ww", "pjo", 0, 64))
-        cp(A("m8"), IND("t8", "olo"), "s")
-        ts(blk("ti", 1), A("pb"), 3, Alu.arith_shift_right)
-        tt(A("wl"), IND("ww", "pjo", 0, 64), A("wh"), Alu.subtract)
-        tt(Z(1), A("pb"), A("idb"), Alu.subtract)
-        cp(A("ohi"), blk("ti", 1))
-        cp(blk("dhl", 0), Z(1))
-        tt(blk("dhl", 1), Z(1), blk("dhl", 0), Alu.subtract)
-        for s3 in range(2):
-            for h in range(8):
-                mm(P(6 + s3, h, 512, 8), gmat(2 * h + s3, 0), A("wh"), True, False)
-                mm(P(6 + s3, h, 512, 8), gmat(2 * h + s3, 0), A("wl"), False, True)
-            tt(A("wt", s3, 1024, 2), P(6 + s3), A("lt", s3, 1024, 2), Alu.add)
-        flip_mm([2, 3], [[blk("dhl", 0)], [blk("dhl", 1)]])
-        flip_out([2, 3], A("dha"))
-        for c0, c1 in CH:
-            tt(A("gp", c0, c1), IND("wt", "ohi", c0, c1), A("m8", c0, c1), Alu.mult)
-            conv2(c0, c1, 4)
-        cp(A("m16"), IND("t16", "vlo"), "s")
-        ts(blk("ti", 3), blk("ti", 2), 4, Alu.arith_shift_right)
-        if rnd == 1:
-            tt(Z(0), blk("dha", 0), blk("dha", 1), Alu.add)
-        cp(A("vhi"), blk("ti", 3))
-        if rnd == 1:
-            tt(blk("af", 2), Z(0), blk("ida", 0), Alu.add)
-        tt(A("eqp"), P(4, 0, 64), blk("ida", 1), Alu.is_equal)
-        cp(A("nwp"), P(4, 64, 128))
-        tt(blk("thl", 0), IND("eqp", "pjo", 0, 64), blk("dha", 0), Alu.mult)
-        tt(blk("thl", 1), IND("eqp", "pjo", 0, 64), blk("dha", 1), Alu.mult)
-        table16(0, [blk("thl", 0), blk("thl", 1)], range(4))
-        table16(1, [blk("thl", 0), blk("thl", 1)], range(4, 8))
-        cp(A("dtab", 0, 256), P(0, 0, 256), "s")
-        tt(S1(1), IND("nwp", "pjo", 0, 64), blk("af", 1), Alu.subtract)
-        tt(S1(2), IND("eqp", "pjo", 0, 64), S1(1), Alu.mult)
-        tt(blk("af", 1), S1(2), blk("af", 1), Alu.add)
-        cp(A("on"), blk("af", 1))
-        cp(A("dtab", 256, 512), P(1, 256, 512))
-        if rnd == 1:
-            for t in (1, 0):
-                dma("y", D("do", None, t), blk("af", t + 1))
-            for t in (1, 0):
-                dma("y", D("lando", r, t), A("af", 64 * t + 64, 64 * t + 128, None, 16 * r, 16 * r + 16))
-            exchange("o")
+        xt, own = "xt%d" % rnd, ["xc", "v16"][rnd]
+        new = ["v16", "w16"][rnd]
+        unit = [(0.0, 1.0), (1025.0, 0.25)][rnd]
+
+        def square(k, c0, c1):
+            act(A("sq", 1024 * k + c0, 1024 * k + c1), A("df", 1024 * k + c0, 1024 * k + c1), Act.Square, *unit)
+
+        def diff(k, off, o0, c0, c1):
+            tt(A("df", 1024 * k + c0, 1024 * k + c1), IND(xt, off, o0 + c0, o0 + c1), A(own, c0, c1), Alu.subtract)
+
+        def penalty(bank, big, e, last=False):
+            mm(P(bank, 0, 64), blk("idn", big, 128), blk("ee", e), e == 0, last)
+
+        cut = 1024 - SHARE[rnd]
+        diff(0, "op", 0, 0, cut)
+        if cut < 1024:
+            cp(A("gn", cut, 1024), IND(xt, "op", cut, 1024), "s")
+            mm(P(3, 0, 1024 - cut), blk("idn", 4, 128), A(own, cut, 1024), True, False)
+            mm(P(3, 0, 1024 - cut), blk("idn", 0, 128), A("gn", cut, 1024), False, True)
+        cp(A("ft", 0, 1024), P(6, 0, 1024), "s")
+        for bank, big in [(0, 2), (1, 3), (2, 3)]:
+            penalty(bank, big, 0)
+        if cut < 1024:
+            act(A("sq", cut, 1024), P(3, 0, 1024 - cut), Act.Square, *unit)
+            conv("sq", 0, cut, 1024, 0, True)
+        square(0, 0, cut)
+        conv("sq", 0, 0, cut, 0, True)
+        penalty(0, 2, 1)
+        penalty(0, 2, 2, True)
+        for c0, c1 in CA:
+            diff(1, "oab", 1024, c0, c1)
+            square(1, c0, c1)
+            conv("sq", 1024, c0, c1, 1, True)
+        for c0, c1 in CB:
+            diff(2, "oab", 0, c0, c1)
+            square(2, c0, c1)
+            conv("sq", 2048, c0, c1, 2, True)
+        cp(A("abd"), IND("ft", "fcd", 64, 192, 0, 1024), ABD)
+        tt(A("ee", 192, 320), A("abd"), A("ld"), Alu.is_equal)
+        penalty(1, 3, 2)
+        penalty(1, 3, 3, True)
+        penalty(2, 3, 1)
+        penalty(2, 3, 4, True)
+        cp(S1(0), P(0, 0, 64), SMALL)
+        tt(S1(1), blk("abd", 0), PD, Alu.subtract)
+        tt(Z(0), P(1, 0, 64), S1(0), Alu.is_lt)
+        tt(S1(2), P(1, 0, 64), S1(0), Alu.min)
+        tt(Z(1), Z(0), S1(1), Alu.mult)
+        tt(A("c1", 1, 192, 3), Z(1), PD, Alu.add)
+        tt(A("c1", 0, 192, 3), blk("abd", 1), A("c1", 1, 192, 3), Alu.subtract)
+        tt(Z(5), P(2, 0, 64), S1(2), Alu.min)
+        tt(A("c0", 1, 192, 3), P(2, 0, 64), S1(2), Alu.is_lt)
+        ts(A("c1", 2, 192, 3), Z(5), A("thf", 0, 1), Alu.is_ge, 8192.0, Alu.mult)
+        chain(A("c2"), A("c0"), A("c1"))
+        cp(blk("kb", 0), A("c2", 2, 192, 3))
+        partner_row()
+        tt(blk("kb", 2), A("c2", 2, 192, 3), blk("kb", 0), Alu.subtract)
+        cp(A("m8", 0, 512), IND("t8", "olo", 0, 512), "s")
+        partner_column()
+        table8("wt", 3, [6, 7], "v")
+        cp(A("m8", 512, 1024), IND("t8", "olo", 512, 1024), "s")
+        table16(3, [PD])
+        cp(blk("ft", 2, 512), P(3), "s")
+        for k in range(3):
+            conv2(*masked("wt", "ohi", "m8", k), 4)
         for k in range(2):
-            cp(blk("gn", k, 512), IND(xt, "on", 512 * k, 512 * k + 512), "s")
-        mm(P(6), blk("idn", 1, 128), blk("xa", 0, 512), True, False)
-        mm(P(6), blk("idn", 0, 128), blk("gn", 0, 512), False, True)
-        for c0, c1 in CH:
-            tt(A("gp", c0, c1), IND("dtab", "vhi", c0, c1), A("m16", c0, c1), Alu.mult)
-            conv("gp", 0, c0, c1, ONES, 2)
-        act(blk("uu", 0, 512), P(6), Act.Identity, 4098.5)
-        mm(P(7), blk("idn", 1, 128), blk("xa", 1, 512), True, False)
-        mm(P(7), blk("idn", 0, 128), blk("gn", 1, 512), False, True)
-        act(blk("uu", 1, 512), P(7), Act.Identity, 4098.5)
-        if rnd == 0:
-            cp(blk("ah", 1), blk("af", 1))
-            tt(Z(0), blk("dha", 0), blk("dha", 1), Alu.add)
-            tt(blk("al", 1), blk("af", 1), blk("ah", 1), Alu.subtract)
-            tt(blk("af", 2), Z(0), blk("ida", 0), Alu.add)
-            table16(3, [blk("ah", 1), blk("al", 1)])
-            cp(blk("ft", 1, 512), P(3), "s")
-        tt(blk("af", 0), P(2, 0, 64), blk("af", 0), Alu.add)
-        if rnd == 0:
-            cp(blk("ah", 0), blk("af", 0))
-            cp(A("ov"), blk("af", 0))
-            tt(blk("al", 0), blk("af", 0), blk("ah", 0), Alu.subtract)
-            link_table(0, 0, "s")
-            link_table(1, 1, "s")
-        else:
-            cp(A("ov"), blk("af", 0))
-            dma("y", D("dv"), blk("af", 0))
-            dma("y", D("landv", r), A("af", 0, 64, None, 16 * r, 16 * r + 16))
-            exchange("v")
-        for hh, (c0, c1) in enumerate(HV):
-            tt(A("v16", c0, c1), IND(xt, "ov", c0, c1), A("uu", c0, c1), Alu.add)
-            ts(A("xa", c0, c1), A("v16", c0, c1), 0.25, Alu.mult, -1025.0, Alu.add)
-            if rnd == 1:
-                dma("y", D("dx%d" % hh), A("xa", c0, c1))
-                dma("s", D("landx%d" % hh, r), A("xa", c0, c1, None, 16 * r, 16 * r + 16))
-        if rnd == 0:
-            jobs = [(q, 0) for q in range(8)] + [(q, 1) for q in range(8)]
-            ring = [2, 3, 4, 6, 7, 1]
+            cp(blk("m16", k, 512), IND("t16", "vlo", 512 * k, 512 * k + 512), "s")
+        tt(S1(3), IND("ft", "fcd", 0, 64), A("idc"), Alu.subtract)
+        split(blk("ah", 2), blk("al", 2), S1(3), ON[2][2])
+        tt(Z(0), two(4, 0), A("idc"), Alu.is_equal)
+        tt(S1(1), two(4, 1), blk("lc", 1), Alu.subtract)
+        for k, nm in enumerate(["ah", "al"]):
+            tt(blk("thl", k), Z(0), blk(nm, 2), Alu.mult)
+        tt(Z(2), Z(0), S1(1), Alu.mult)
+        tt(blk("lc", 1), Z(2), blk("lc", 1), Alu.add)
+        cp(A("on"), blk("lc", 1))
+        for bk in range(2):
+            table16(bk, [blk("thl", 0), blk("thl", 1)], range(4 * bk, 4 * bk + 4))
+            cp(blk("dtab", bk, 256), P(bk, 256 * bk, 256 * bk + 256), ON[1][bk])
+        turns = [to[k] for k in (1, 2, 3, 0)]
+        h0 = turns[0][0] // 4
 
-            def rebuild(k0, k1, es):
-                for k in range(k0, k1):
-                    q, hh = jobs[k]
-                    e = es[(k - k0) % len(es)]
-                    if e != "V":
-                        mm(P(ring[k % 6]), blk("rep", q, 128), blk("xa", hh, 512), True, True)
-                    if e != "-":
-                        cp(blk("xt1", 2 * q + hh, 512), P(ring[k % 6]), e.lower())
+        def ahead(hh):
+            cp(blk("gn", hh, 512), IND(xt, "on", 512 * hh, 512 * hh + 512), "s")
+            mm(P(6 + hh), blk("idn", 1, 128), blk(own, hh, 512), True, False)
+            mm(P(6 + hh), blk("idn", 0, 128), blk("gn", hh, 512), False, True)
 
-            cp(A("op"), blk("af", 2))
-            rebuild(0, 9, "vsssss--s")
-            for k in range(3):
-                link_chunk(k, 0)
-            rebuild(6, 8, "V")
-            rebuild(9, 11, "s")
-            link_lists(0)
-            cp(A("oab"), IND("abp", "pjo", 0, 128))
-            rebuild(11, 16, "vs")
+        def ahead_out(hh):
+            act(blk("uu", hh, 512), P(6 + hh), Act.Identity, [4098.5, 8194.0][rnd])
+
+        def smooth(c0, n):
+            tt(A(new, c0, c0 + n), IND(xt, "ov", c0, c0 + n), A("uu", c0, c0 + n), Alu.add)
+
+        def behind(c0, n, bank):
+            tt(A("gp", c0, c0 + n), IND("dtab", "vhi", c0, c0 + n), A("m16", c0, c0 + n), Alu.mult)
+            conv("gp", 0, c0, c0 + n, bank)
+            tt(A("lc", c0 // 16, (c0 + n) // 16), P(bank, c0 // 16, (c0 + n) // 16), A("lc", c0 // 16, (c0 + n) // 16), Alu.add)
+            cp(A("ov", c0 // 16, (c0 + n) // 16), A("lc", c0 // 16, (c0 + n) // 16))
+
+        ahead(h0)
+        ahead_out(h0)
+        ahead(1 - h0)
+        ahead_out(1 - h0)
+        if rnd == 0:
+            for k, (c0, n) in enumerate([(512 * h0, 512), (512 - 512 * h0, 512)]):
+                behind(c0, n, 2 + k)
+            split(blk("ah", 0), blk("al", 0), blk("lc", 0))
             table16(1, [blk("ah", 0), blk("al", 0)])
-            cp(blk("ft", 0, 512), P(1), "s")
-            cp(A("bfl", 0, 128), IND("ft", "flo", 0, 128, 1024), "s")
+            smooth(512 * h0, 256)
+            smooth(512 * h0 + 256, 256)
+            smooth(512 - 512 * h0, 512)
+            table16(0, [blk("lc", 1)])
+            for t in range(2):
+                cp(blk("ft", t, 512), P(t), "s")
+            cp(A("ld"), IND("ft", "fcd", 64, 192, 0, 1024), "a")
+            partner_links()
+            qs = list(range(4 * h0, 4 * h0 + 4)) + list(range(4 - 4 * h0, 8 - 4 * h0))
+            points("xt1", "v16", qs[:6], [2, 6, 2, 6, 0, 2], WHOLE[1], -4100.0)
+            partner_lists()
+            cp(A("op"), IND("ft", "fcd", 0, 64))
+            points("xt1", "v16", qs[6:], [0, 2], WHOLE[1][6:], -4100.0)
+            closed()
+            prv_place()
+        else:
+            cp(blk("lo", 2), IND("ft", "fda", 0, 64), "s")
+            dma("y", D("dvs"), blk("lo", 2))
+            dma("y", D("landv", r), A("lo", 128, 192, None, 16 * r, 16 * r + 16))
+            exchange("v")
+            home = T.back[:, 128 * r:128 * r + 128]
+            def successors(bank, q):
+                table16(bank, [blk("lc", 1)])
+                cp(blk("ft", 0, 512), P(bank), q)
+                cp(blk("lo", 1), IND("ft", "fac", 0, 64, 0, 512), q)
+                dma("y", D("dos", None, 1), blk("lo", 1))
 
-    exchange("x0")
-    exchange("x1")
-    dma("y", X(T.yn[:]), D("lando", None, 0))
-    dma("s", X(T.yp[:]), D("lando", None, 1))
-    dma("y", X(T.yv[:]), D("landv"))
-    for hh, (c0, c1) in enumerate(HV):
-        dma("g", X(T.yx[:, c0:c1]), D("landx%d" % hh))
+            if TAIL == 10:
+                successors(4, "s")
+                c1 = 128 * turns[0][0]
+                behind(c1, 256, 2)
+                for c0, n in [(c1 + 256, 768 - c1), (0, c1)]:
+                    if n:
+                        behind(c0, n, 3 if c0 else 1)
+            else:
+                for k in range(4):
+                    behind(128 * turns[k][0], 256, 2 + k % 2)
+            for k in range(4):
+                qs, bk = turns[k], [4, 6 + h0, 4, 7 - h0][k]
+                c0 = 128 * qs[0]
+                smooth(c0, 256)
+                mm(P(bk, 0, 256), blk("prm", 1, 128), A(new, c0, c0 + 256))
+                if k < 3:
+                    cp(A("so", c0, c0 + 256), P(bk, 0, 256), "a", -1025.0)
+                    if k < 2 or not JOIN:
+                        send(pieces("so", qs[0], qs, home, "br%d" % (k + 1)), [A("lo")] if k == 1 else [])
+                else:
+                    j = qs.index(mate)
+                    cp(blk("so", mate, 128), P(bk, 128 * j, 128 * j + 128), "a", -1025.0)
+                    send((pieces("so", to[3][0], to[3], home, "br3") if JOIN else []) + [(mate, near, blk("so", mate, 128), home, "brm")])
+                    cp(blk("xo", r, 128), P(bk, 128 - 128 * j, 256 - 128 * j), "a", -1025.0)
+                if k == 0:
+                    split(blk("ah", 0), blk("al", 0), blk("lc", 0))
+                    table16(0, [blk("ah", 0), blk("al", 0)])
+                    if TAIL != 10:
+                        successors(1, "a")
+                    cp(blk("ft", 1, 512), P(0), "a")
+                    cp(blk("lo", 0), IND("ft", "fac", 64, 128, 0, 1024), "a")
+                    dma("y", D("dos", None, 0), blk("lo", 0))
+                    for t in (1, 0):
+                        dma("y", D("lando", r, t), A("lo", 64 * t, 64 * t + 64, None, 16 * r, 16 * r + 16))
+            exchange("o")
+
+    arrive([blk("back", mate, 128)], "brm", len(near))
+    for k in (1, 2, 3):
+        arrive([blk("back", q, 128) for q in fr[k]], "br%d" % k, 2 * hf)
+    dma("y", X(T.yx[16 * r:16 * r + 16, :]), blk("xo", r, 128))
+    dma("y", X(T.yp[:]), D("landv"))
+    for j, qs in enumerate([fr[1], fr[2], [mate], fr[3]] if JOIN else [fr[1], [mate], fr[2], fr[3]]):
+        cp(A("xo", 128 * qs[0], 128 * qs[-1] + 128), A("back", 128 * qs[0], 128 * qs[-1] + 128))
+        for q in qs:
+            dma("ys"[q % 2], X(T.yx[16 * q:16 * q + 16, :]), blk("xo", q, 128))
+    dma("s", X(T.yn[:]), D("lando", None, 1))
+    dma("y", X(T.yv[:]), D("lando", None, 0))
 
     def meet(a, b):
+        if a[5] == b[5] and a[3] % a[5] != b[3] % b[5]:
+            return False
         return a[0] == b[0] and a[1] < b[2] and b[1] < a[2] and a[3] < b[4] and b[3] < a[4]
 
+    def follows():
+        seen, last = {}, {}
+        for i, o in enumerate(ops):
+            dep = set()
+            for k, wr in [(k, True) for k in o["w"]] + [(k, False) for k in o["r"]]:
+                for j, kk, ww in seen.get(k[0], []):
+                    bank = k[0].startswith("ps") and (ops[j]["q"] != o["q"] or o["q"] in "pa")
+                    if bank or ((wr or ww) and meet(k, kk)):
+                        dep.add(j)
+            if o["kind"] == "a":
+                dep = {o["like"]}
+            if o["kind"] in "dr" or o["q"] == "g":
+                if o["q"] in last:
+                    o["behind"] = last[o["q"]]
+                last[o["q"]] = i
+            o["dep"] = dep
+            for k in o["w"]:
+                seen.setdefault(k[0], []).append((i, k, True))
+            for k in o["r"]:
+                seen.setdefault(k[0], []).append((i, k, False))
+
+    def place(rank, back, LOOK):
+        n = len(ops)
+        after, left, ready, at, on_q = [[] for _ in ops], [0] * n, [0] * n, [0] * n, [None] * n
+        for i, o in enumerate(ops):
+            for j in o["dep"] | ({o["behind"]} if "behind" in o else set()):
+                a, b = (i, j) if back else (j, i)
+                after[a].append(b)
+                left[b] += 1
+        free, wire, done, bind, begin, latest = {q: 0 for q in Q}, [0], [], [None] * n, [0] * n, {}
+        todo = [i for i in range(n) if left[i] == 0]
+        while todo:
+            can = [(max(ready[i], free.get(q, 0)), i, q) for i in todo for q in (["s", "v"] if ops[i]["q"] == "a" else [ops[i]["q"]])]
+            t0, _, q0 = min(can, key=lambda c: c[0])
+            due = 1e9
+            for t, i, q in sorted([c for c in can if c[2] == q0], key=lambda c: (rank[c[1]], c[1])):
+                o = ops[i]
+                hold = o["hold"][q] if isinstance(o["hold"], dict) else o["hold"]
+                if t <= t0 + LOOK and t + hold <= due + SLACK:
+                    break
+                if t > t0 + LOOK and o["q"] not in ("a", None):
+                    due = min(due, t)
+            else:
+                free[q0] = due
+                continue
+            todo.remove(i)
+            done.append(i)
+            on_q[i], begin[i] = q, t
+            if t > ready[i]:
+                bind[i] = latest.get(q)
+            latest[q] = i
+            if back and "wire" in o:
+                wire[0] = t = max(t, wire[0]) + o["wire"]
+            if q is not None:
+                free[q] = t + hold
+            end = t + hold
+            if not back:
+                end += o["flight"]
+                if "wire" in o:
+                    wire[0] = end = max(end, wire[0]) + o["wire"]
+            at[i] = end
+            for j in after[i]:
+                e = ops[j]
+                wake = 0 if q == "p" == e["q"] else WAKE
+                if back:
+                    due = end + wake + (e["flight"] if j in o["dep"] else 0)
+                else:
+                    due = end + wake if i in e["dep"] else t
+                if due > ready[j]:
+                    ready[j], bind[j] = due, i
+                left[j] -= 1
+                if left[j] == 0:
+                    todo.append(j)
+        return max(at), done, on_q, [-t for t in at], bind, begin
+
+    follows()
+    above = []
+    for o in ops:
+        m = 0
+        for j in o["dep"]:
+            m |= above[j]
+        o["dep"] = {j for j in o["dep"] if not m >> j & 1}
+        above.append(m | sum(1 << j for j in o["dep"]))
+    best = tried = place(list(range(len(ops))), False, LOOKS[0])
+    for look in LOOKS:
+        tried = place(place(best[3], True, look)[3], False, look)
+        best = min(best, tried, key=lambda b: b[0])
+    for i, o in enumerate(ops):
+        o["any"] = o["hold"] if o["q"] == "a" else None
+        o["q"] = best[2][i]
+        o["hold"] = o["hold"][o["q"]] if isinstance(o["hold"], dict) else o["hold"]
+
+    def replay(order, wake, more):
+        free, last, end, bind, wire = {}, {}, {}, {}, 0
+        for i in order:
+            o = ops[i]
+            q = o["q"]
+            t, bind[i] = (free.get(q, 0), last.get(q)) if q else (0, None)
+            for j in o["dep"]:
+                e = end[j] + (0 if q == "p" == ops[j]["q"] else wake)
+                if e > t:
+                    t, bind[i] = e, j
+            free[q], last[q] = t + o["hold"] + more.get(q, 0), i
+            end[i] = free[q] + o["flight"]
+            if "wire" in o:
+                wire = end[i] = max(end[i], wire) + o["wire"]
+        return max(end.values()) + EARLY * sum(end.values()), bind, max(end, key=end.get)
+
+    def length(order):
+        return sum(replay(order, wake, more)[0] for wake, more in SPREAD)
+
+    order, now = best[1], length(best[1])
+    for k in range(SWEEPS):
+        _, bind, i = replay(order, *SPREAD[k % len(SPREAD)])
+        while bind[i] is not None:
+            j = bind[i]
+            o = ops[i]
+            if o["any"]:
+                was = o["q"]
+                o["q"] = "s" if was == "v" else "v"
+                o["hold"] = o["any"][o["q"]]
+                if length(order) < now:
+                    now = length(order)
+                else:
+                    o["q"], o["hold"] = was, o["any"][was]
+            if ops[i]["q"] == ops[j]["q"] and ops[i]["q"] in "vsp" and ops[i]["kind"] == "c" == ops[j]["kind"] and j not in ops[i]["dep"]:
+                a, b = order.index(j), order.index(i)
+                tied = {j}
+                for x in order[a + 1:b + 1]:
+                    if ops[x]["dep"] & tied or ops[x].get("behind") in tied:
+                        tied.add(x)
+                if i not in tied:
+                    other = order[:a] + [x for x in order[a:b + 1] if x not in tied] + [x for x in order[a:b + 1] if x in tied] + order[b + 1:]
+                    if length(other) < now:
+                        order, now = other, length(other)
+            i = j
+    ops = [ops[i] for i in order]
     clock = {q: {} for q in Q}
     seen = {}
     for i, o in enumerate(ops):
@@ -539,7 +762,7 @@ def rank_program(g, core, T, topo):
             e = ops[j]
             Q[o["q"]].wait_ge(T.sem[e["sem"]], e["at"])
             waited[e["sem"]] = max(waited.get(e["sem"], 0), e["at"])
-        ins = o["fn"]()
+        ins = o["fn"][o["q"]]() if isinstance(o["fn"], dict) else o["fn"]()
         if o["sig"] and o["kind"] != "r":
             ins.then_inc(T.sem[o["sem"]], o["n"])
     for sem in count:

from concourse.bass import DstId, RemoteDMATransfer
from concourse.mybir import AluOpType, ActivationFunctionType

F, B, I, U, H = "float32", "bfloat16", "int32", "uint16", "float16"
SCRATCH = {}
for _d, _names in {
    I: "xi:1024 pi:16 thi:4 la:192 ti:128 tv:320",
    B: "sb:1024 sx:1024 xc:1024 gn:1024 xt0:8192 xt1:8192 rep:1024 km:512 idn:1664 fb:128 prm:256 i128:128 i1:128 ip:256 kb:256 "
       "ks:256 thl:128 abh:128 abl:128 ah:192 al:192 ee:320 so:1024 back:1024",
    F: "df:3072 sq:3072 uu:1024 gp:1024 m8:1024 m16:1024 lt:1024 wt:1024 dtab:512 ft:1536 xo:1024 repf:1024 pu:8 i16:16 pf:16 "
       "cc:8 kc:4 f0:48 idc0:64 idc:64 idd:64 sel:40 i16b:16 t8:8 t16:16 thf:4 lc:128 ld:128 c0:192 c1:192 c2:192 abd:128 s1:512 lo:192",
    U: "fac:24 fcd:12 fda:4 op:64 oab:128 olo:64 ohi:64 vlo:64 vhi:64 on:64 ov:64",
    H: "v16:1024 w16:1024 fh:64",
}.items():
    for _w in _names.split():
        SCRATCH[_w.split(":")[0]] = ("sbuf", [128, int(_w.split(":")[1])], _d)
for _n, _w, _d in [("l", 16, I), ("p", 8, I), ("o", 16, F), ("v", 8, F)]:
    SCRATCH["d" + _n + "s"] = ("dram", [8, 128, _w], _d)
    SCRATCH["land" + _n] = ("dram", [8, 128, _w], _d)
for _k in range(4):
    SCRATCH["pq%d" % _k] = ("psum", [128, 1024], F)
SEMAPHORES = (["cv", "cs", "cp", "cg"] + ["d%d" % k for k in range(60)] + ["arl", "arp", "aro", "arv", "arm", "brm"]
              + ["ar%d" % k for k in range(1, 4)] + ["br%d" % k for k in range(1, 4)] + ["sn%d" % k for k in range(14)])

START, GATHER, WAKE, LOOKS, SLACK = {"v": 45, "s": 160}, 1.5, 110, [120, 60, 200, 90, 150], 2000
LOCAL, REMOTE, WIRE, CALL, FIRST = 2300, 2600, 1300, 360, 2800
WHOLE = [[0] * 4, [0] * 8]
SHARE = [384, 384]
SMALL, ABD, BOOSTS, GATE, TAIL, LATER = "v", "a", 0, 3, 7, 1200
EARLY = 0.0002
SWEEPS, SPREAD = 6, [(70, {}), (120, {"v": 15, "s": -20})]
PAT, JOIN = 0, 0
ON = ["aa", "vv", "vvv"]
CA = [(0, 512), (512, 1024)]
CB = [(0, 640), (640, 1024)]
CH = [(0, 512), (512, 768), (768, 1024)]


def rank_program(g, core, T, topo):
    r = T.rank_of(core)
    if r is None:
        return
    cores = list(T.cores)
    ops = []
    Q = {"v": g.vector, "s": g.scalar, "p": g.tensor, "g": g, "y": g.sync}
    Alu, Act = AluOpType, ActivationFunctionType

    def A(name, c0=None, c1=None, st=None, p0=0, p1=128):
        t = T[name]
        if c0 is None:
            c0, c1 = 0, t.shape[1]
        ap = t[p0:p1, c0:c1:st] if st else t[p0:p1, c0:c1]
        return ap, [(name, p0, p1, c0, c1, st or 1)], len(range(c0, c1, st or 1)), SCRATCH[name]

    def D(name, k=None, t=None):
        b = T[name]
        if t is None:
            ap = b[:] if k is None else b[k]
        else:
            n = 1024 // b.shape[2]
            ap = b[:, n * t:n * t + n, :] if k is None else b[k, n * t:n * t + n, :]
        return ap, [(name, 0 if k is None else k, 8 if k is None else k + 1, 0 if t is None else t, 4 if t is None else t + 1, 1)]

    def X(ap):
        return ap, []

    def IND(win, off, c0=0, c1=1024, w0=None, w1=None):
        w, o = A(win, w0, w1), A(off, c0 // 16, c1 // 16)
        return w[0].indirect(o[0]), w[1] + o[1], c1 - c0, None

    def add(q, fn, outs, ins, hold, kind="c", sem=None, n=0, flight=0):
        ops.append({"q": q, "fn": fn, "w": [k for o in outs for k in o[1]], "r": [k for o in ins for k in o[1]],
                    "kind": kind, "sem": sem, "n": n, "hold": hold, "flight": flight})

    def col(s):
        return [s] if isinstance(s, tuple) else []

    def val(s):
        return s[0] if isinstance(s, tuple) else s

    def cycles(q, a, rate):
        return 70 + GATHER * a[2] if a[3] is None else max(64, START[q] + rate * a[2])

    def short(*xs):
        return 0.5 if all(x[3] and x[3][2] in (B, H, U) for x in xs) else 1

    def tt(o, a, b, op):
        add("v", lambda: g.vector.tensor_tensor(o[0], a[0], b[0], op), [o], [a, b],
            cycles("v", a, 2 if a[3] and a[3][0] == b[3][0] else 1))

    def ts(o, a, s1, op0, s2=None, op1=None):
        if op1 is None:
            add("v", lambda: g.vector.tensor_scalar(o[0], a[0], val(s1), None, op0), [o], [a] + col(s1), cycles("v", a, short(o, a)))
        else:
            add("v", lambda: g.vector.tensor_scalar(o[0], a[0], val(s1), val(s2), op0, op1), [o], [a] + col(s1) + col(s2),
                cycles("v", a, short(o, a)))

    def chain(o, a, b):
        add("v", lambda: g.vector.tensor_tensor_scan(o[0], a[0], b[0], 0.0, Alu.mult, Alu.add), [o], [a, b], cycles("v", a, 1))

    def act(o, a, f, bias=0.0, scale=1.0):
        add("s", lambda: g.scalar.activation(o[0], a[0], f, bias=bias, scale=scale), [o], [a], cycles("s", a, 1))

    def cp(o, a, q="v", bias=None):
        if bias is None:
            fns = {"v": lambda: g.vector.tensor_copy(o[0], a[0]), "s": lambda: g.scalar.activation(o[0], a[0], Act.Copy)}
        else:
            fns = {"v": lambda: g.vector.tensor_scalar(o[0], a[0], bias, None, Alu.add),
                   "s": lambda: g.scalar.activation(o[0], a[0], Act.Identity, bias=bias)}
        add(q, fns, [o], [a], {"v": cycles("v", a, short(o, a)), "s": cycles("s", a, 1)})

    def mm(o, l, m, st=True, sp=True):
        add("p", lambda: g.tensor.matmul(o[0], l[0], m[0], st, sp), [o], [l, m], max(64, m[2]) * (2.4 if m[3][2] == F else 0.6))

    def iota(o, pat, base, cm, flt=True, after=()):
        if flt:
            add("g", lambda: g.iota(o[0], pat, base, cm, allow_small_or_imprecise_dtypes=True), [o], list(after), 160 + 2 * o[2])
        else:
            add("g", lambda: g.iota(o[0], pat, base, cm), [o], [], 160 + 2 * o[2])

    nd = [0]

    def dma(q, o, a, more=0):
        sem = "d%d" % nd[0]
        nd[0] += 1
        add(q, lambda: Q[q].dma_start(o[0], a[0]), [o], [a], 60, "d", sem, 16, LOCAL + more)

    ns, sent = [0], {}

    def bits(es):
        return sum(1 << e for e in es)

    def send(items, after=()):
        sem = "sn%d" % ns[0]
        ns[0] += 1
        trs = []
        for q, es, src, dst, rs in items:
            rid, pid, _ = topo.addr(cores[q])
            trs.append(RemoteDMATransfer(dst_ids=[DstId(rid=rid, pnc=pid)], dma_engine_mask=bits(es),
                                         remote_sem=T.sem[rs], src=src[0], dst=dst))
        add("g", lambda: g.remote_dma_fused(trs, local_sem=T.sem[sem]), [], [i[2] for i in items] + list(after),
            FIRST if ns[0] == 1 else CALL, "r", sem, sum(len(i[1]) for i in items), REMOTE)
        if len(items) > 1:
            ops[-1]["wire"] = WIRE if SCRATCH[items[0][2][1][0][0]][0] == "sbuf" else WIRE // 3
        for i in items:
            sent[i[4]] = len(ops) - 1

    def arrive(outs, sem, n):
        add(None, None, outs, [], 0, "a", sem, n)
        ops[-1]["like"] = sent[sem]

    chips = sorted(set(topo.chip(c) for c in cores))
    on = [[q for q in range(8) if topo.chip(cores[q]) == ch] for ch in chips]
    ci = chips.index(topo.chip(core))
    mate = [q for q in on[ci] if q != r][0]
    to = [on[(ci + k) % 4] for k in range(4)]
    fr = [on[(ci - k) % 4] for k in range(4)]
    far = topo.engines(core, cores[to[1][0]])
    near = [e for e in topo.engines(core, cores[mate]) if e not in far]
    hf = len(far) // 2
    others = to[1] + to[2] + to[3]
    solo = far[0::2] + far[1::2]

    def exchange(n):
        src, dst, sem = "d" + n + "s", "land" + n, "ar" + n
        send([(mate, near[:2], D(src, mate), T[dst][r], sem)]
             + [(q, [solo[j]], D(src, q), T[dst][r], sem) for j, q in enumerate(others)])
        arrive([D(dst, q) for q in range(8) if q != r], sem, 8)

    def P(k, c0=0, c1=512, st=1):
        b0 = 512 * (k % 2)
        return (T["pq%d" % (k // 2)][:, b0 + c0:b0 + c1:st], [("ps%d" % (k + j), 0, 128, c0, c1, st) for j in range(1 + (c1 > 512))],
                len(range(c0, c1, st)), SCRATCH["pq0"])

    def blk(name, k, n=64):
        return A(name, n * k, n * k + n)

    def S1(k):
        return blk("s1", k)

    def Z(k):
        return P(5, 64 * k, 64 * k + 64)

    SHR, AND = Alu.arith_shift_right, Alu.bitwise_and

    lists = [T.prv, T.nxt, T.ptn]
    for t in range(3):
        dma("y" if t % 2 == 0 else "s", D("dls", None, t) if t < 2 else D("dps"), X(lists[t][:]))
    order = to[1] + [mate] + to[2] + to[3] + [r]
    for j, q in enumerate(order):
        dma("s" if j % 2 == 0 else "y", blk("xi", j, 128), X(T.x[16 * q:16 * q + 16, :]), 700 + 350 * j)
    for t in range(3):
        dma("s", D("landl", r, t) if t < 2 else D("landp", r), X(lists[t][16 * r:16 * r + 16, :]))
    for k in range(8):
        dma("y", A("thi", 0, 1, None, 16 * k, 16 * k + 16), X(T.th[16 * r:16 * r + 16, :]), 9000)

    def pf(k):
        return A("pf", k, k + 1)

    def cc(k):
        return A("cc", k, k + 1)

    iota(A("pu"), [[-16, 8]], 0, 1)
    iota(A("ip", 0, 128), [[1, 8], [8, 16]], 0, 0)
    iota(A("i1"), [[0, 8], [1, 16]], 0, 0)
    iota(A("pi", 0, 1), [[0, 1]], 0, 1, False)
    iota(A("i128"), [[1, 128]], 0, 0)
    iota(A("i16"), [[1, 16]], 0, 0)
    exchange("l")
    if PAT == 0:
        exchange("p")
    ts(blk("prm", 0, 128), blk("ip", 0, 128), A("pu", 0, 1), Alu.is_equal)

    def pieces(src, j, qs, dst, sem):
        return [(qs[0], far[:hf], blk(src, j, 128), dst, sem), (qs[1], far[hf:], blk(src, j + 1, 128), dst, sem)]

    def turn(j0, j1, bank, out):
        cp(A("sb", 128 * j0, 128 * j1), A("xi", 128 * j0, 128 * j1))
        mm(P(bank, 0, 128 * (j1 - j0)), blk("prm", 0, 128), A("sb", 128 * j0, 128 * j1))
        cp(out, P(bank, 0, 128 * (j1 - j0)), "s")

    mine = T.xc[:, 128 * r:128 * r + 128]
    turn(0, 3, 0, A("sx", 0, 384))
    send(pieces("sx", 0, to[1], mine, "ar1") + [(mate, near, blk("sx", 2, 128), mine, "arm")])
    if PAT == 1:
        exchange("p")
    turn(3, 5, 1, A("sx", 384, 640))
    if GATE == 3:
        send(pieces("sx", 3, to[2], mine, "ar2"))
    turn(5, 7, 6, A("sx", 640, 896))
    turn(7, 8, 7, blk("xc", r, 128))
    iota(A("f0", 0, 12), [[512, 3], [128, 4]], 0, 0)
    iota(A("f0", 12, 24), [[-512, 3], [16, 4]], 1024, 0)
    iota(A("f0", 24, 28), [[2, 4]], 1024, 0)
    iota(A("idd"), [[1024, 8], [128, 8]], 0, 1)
    iota(A("idc0"), [[1024, 8], [16, 8]], 0, 1)
    iota(A("ip", 128, 256), [[1, 16], [16, 8]], 0, 0, True, [D("landl"), D("landp")])
    ops[-1]["flight"] = 20000
    if GATE == 2:
        send(pieces("sx", 3, to[2], mine, "ar2"))
    send(pieces("sx", 5, to[3], mine, "ar3"))
    iota(A("c1"), [[0, 64], [1, 3]], 0, 0)
    ops[-1]["flight"] = 6000
    arrive([blk("xc", mate, 128)], "arm", len(near))
    for k in (1, 2, 3):
        arrive([blk("xc", q, 128) for q in fr[k]], "ar%d" % k, 2 * hf)
        ops[-1]["flight"] = LATER if k == 2 else 0

    for k in range(8):
        ts(blk("rep", k, 128), A("i1"), A("pu", k, k + 1), Alu.is_equal)
    for k, (sh, m) in enumerate([(0, 7), (0, 15), (3, 15), (4, 7), (3, 1), (5, 1), (2, 7), (0, 3)]):
        ts(A("pi", k + 1, k + 2), A("pi", 0, 1), sh, SHR, m, AND)
    cp(A("pf", 0, 9), A("pi", 0, 9))
    cp(A("repf"), A("rep"), "s")
    ts(cc(6), pf(6), 8.0, Alu.mult, pf(7), Alu.add)
    ts(A("kc"), A("i16", 0, 4), pf(8), Alu.not_equal, 100.0, Alu.mult)
    for k, v in enumerate([1.0, 2.0, 2.0 ** 21, 2.0 ** 23, -1.0, 1 / 16, 7 / 16, -63 / 128]):
        ts(blk("idn", k, 128), A("i128"), pf(0), Alu.is_equal, v, Alu.mult)
    ts(A("kc"), A("kc"), cc(6), Alu.add)
    ts(cc(0), pf(5), 64.0, Alu.mult, pf(1), Alu.add)
    ts(cc(2), pf(5), 64.0, Alu.mult, pf(4), Alu.add)
    ts(cc(3), pf(1), 64.0, Alu.mult, pf(4), Alu.add)
    ts(cc(4), pf(1), 64.0, Alu.mult, pf(5), Alu.add)
    for j in range(4):
        ts(blk("km", j, 128), A("i1"), A("kc", j, j + 1), Alu.is_equal)
    ts(cc(0), pf(4), 8.0, Alu.mult, cc(0), Alu.add)
    ts(cc(2), pf(1), 8.0, Alu.mult, cc(2), Alu.add)
    ts(cc(3), pf(5), 8.0, Alu.mult, cc(3), Alu.add)
    ts(cc(4), pf(4), 8.0, Alu.mult, cc(4), Alu.add)
    ts(cc(5), pf(4), 112.0, Alu.mult)
    ts(A("t8"), A("i16", 0, 8), pf(1), Alu.is_equal)
    ts(A("t16"), A("i16"), pf(2), Alu.is_equal)
    ts(A("sel", 0, 16), A("i16"), pf(3), Alu.is_equal)
    ts(A("sel", 16, 24), A("i16", 0, 8), pf(4), Alu.is_equal)
    ts(A("fac", 0, 12), A("f0", 0, 12), cc(0), Alu.add)
    ts(A("fac", 12, 24), A("f0", 0, 12), cc(2), Alu.add)
    ts(A("fcd"), A("f0", 12, 24), cc(3), Alu.add)
    ts(A("fda"), A("f0", 24, 28), cc(4), Alu.add)
    ts(A("idc"), A("idc0"), cc(5), Alu.add)

    ts(A("c0"), A("c1"), 0.5, Alu.mult)

    ONES, PD = A("sel", 16, 24), A("c2", 1, 192, 3)

    def conv(src, base, c0, c1, bank, opened=False, last=False):
        for b in range(c0 // 128, c1 // 128):
            mm(P(bank, 8 * b, 8 * b + 8), A(src, base + 128 * b, base + 128 * b + 128), ONES, not opened, not opened or (last and b == 7))

    def conv2(c0, c1, bank):
        for b in range(c0 // 128, c1 // 128):
            mm(P(bank, 16 * b, 16 * b + 16), A("gp", 128 * b, 128 * b + 128), A("sel", 0, 16))

    def two(name, k):
        return P(name, k, 128, 2) if isinstance(name, int) else A(name, k, 128, 2)

    def table16(bank, pts, qs=range(8)):
        for q in qs:
            for j, pt in enumerate(pts):
                mm(P(bank, 64 * q, 64 * q + 64), blk("repf" if pt[3][2] == F else "rep", q, 128), pt, j == 0, j == len(pts) - 1)

    def split(h, lo, src, q="v"):
        cp(h, src, q)
        tt(lo, src, h, Alu.subtract)

    def table8(out, bank, banks, q):
        for e in range(2):
            mm(P(bank, 128 * e, 128 * e + 128), A("kb", e, 256, 2), blk("idn", 0, 128))
        cp(A("ks"), P(bank, 0, 256), q)
        for hh, bk in enumerate(banks):
            for j in range(2):
                mm(P(bk, 256 * j, 256 * j + 256), blk("km", 2 * hh + j, 128), A("ks"))
            cp(blk(out, hh, 512), P(bk), "a" if out == "lt" else ON[0][hh])

    def masked(tab, off, mask, k):
        c0, c1 = CH[k]
        tt(A("gp", c0, c1), IND(tab, off, c0, c1), A(mask, c0, c1), Alu.mult)
        return c0, c1

    def partner_row():
        ts(A("olo"), PD, 2.0 ** -10, Alu.mult, -0.49951171875, Alu.add)

    def partner_column():
        cp(blk("ti", 0), PD)
        ts(blk("ti", 1), blk("ti", 0), 1023, AND)
        cp(A("ohi"), blk("ti", 1))

    def partner_links():
        split(A("kb", 0, 128), A("kb", 128, 256), A("ld"))
        table8("lt", 4, [0, 1], "v")
        for k in range(3):
            conv2(*masked("lt", "ohi", "m8", k), 4)

    def partner_lists():
        split(A("abh"), A("abl"), P(4, 0, 128), ON[2][1])
        cp(blk("oab", 1), two(4, 1))
        cp(blk("oab", 0), two(4, 0))
        for t in (1, 0):
            table16(6 + t, [two("abh", t), two("abl", t)])

    def closed():
        tt(blk("ee", 0), PD, A("idd"), Alu.is_equal)
        tt(blk("ee", 1), PD, blk("ld", 1), Alu.is_equal)
        tt(blk("ee", 2), PD, blk("ld", 0), Alu.is_equal)

    def fields(n):
        ts(A("fh"), n, 16400 - 7.5, Alu.add)
        ts(blk("fb", 0), n, 132096 - 511.5, Alu.add)
        ts(blk("fb", 1), n, 16512 - 63.5, Alu.add)

    def prv_place():
        fields(blk("ld", 0))
        for j, (w, x) in enumerate([(0, blk("kb", 0)), (0, blk("kb", 2)), (4, A("fh"))]):
            mm(Z(6), blk("idn", w, 128), x, j == 0, j == 2)
        for j, (w, x) in enumerate([(5, A("fh")), (6, blk("fb", 1)), (7, blk("fb", 0))]):
            mm(Z(7), blk("idn", w, 128), x, j == 0, j == 2)
        ts(A("vlo"), Z(6), 16400.0, Alu.add)
        ts(A("vhi"), Z(7), 132096 * 63 / 128 - 16512 * 7 / 16 - 16400 / 16, Alu.add)

    def points(xt, src, qs, pairs, whole, bias=None):
        for q, bk, w in zip(qs, pairs, whole):
            for b in range(8):
                mm(P(bk + b // 4, 128 * (b % 4), 128 * (b % 4) + 128), blk("rep", b, 128), blk(src, q, 128))
                if b == 7 and w:
                    cp(blk(xt, q, 1024), P(bk, 0, 1024), "s", bias)
                elif b % 4 == 3 and not w:
                    cp(blk(xt, 2 * q + b // 4, 512), P(bk + b // 4), "a", bias)

    points("xt0", "xc", [r], [2], [0])
    for t in range(3):
        dma("y", blk("la", t), D("landl", None, t) if t < 2 else D("landp"))
    points("xt0", "xc", [mate] + fr[1], [6, 2, 6], [0, 0, 0])
    split(A("ah", 0, 128), A("al", 0, 128), A("la", 0, 128))
    split(blk("ah", 2), blk("al", 2), blk("la", 2))
    for t, bk in [(0, 0), (1, 1), (2, 4)]:
        table16(bk, [blk("ah", t), blk("al", t)])
        cp(blk("ft", t, 512), P(bk), "a")
    cp(A("ld"), IND("ft", "fac", 192, 320, 0, 1024), "a")
    cp(PD, IND("ft", "fac", 320, 384))
    partner_row()
    for c0 in (0, 512):
        cp(A("m8", c0, c0 + 512), IND("t8", "olo", c0, c0 + 512), "s")
    partner_column()
    partner_links()
    cp(A("op"), IND("ft", "fac", 128, 192))
    points("xt0", "xc", fr[2] + fr[3], [2, 6, 2, 0], WHOLE[0])
    partner_lists()
    cp(A("lc"), IND("ft", "fac", 0, 128, 0, 1024), "a")
    closed()
    prv_place()
    ts(blk("prm", 1, 128), blk("ip", 1, 128), pf(0), Alu.is_equal, 0.0625, Alu.mult)
    cp(A("thf", 0, 1), A("thi", 0, 1))

    for rnd in range(2):
        xt, own = "xt%d" % rnd, ["xc", "v16"][rnd]
        new = ["v16", "w16"][rnd]
        unit = [(0.0, 1.0), (1025.0, 0.25)][rnd]

        def square(k, c0, c1):
            act(A("sq", 1024 * k + c0, 1024 * k + c1), A("df", 1024 * k + c0, 1024 * k + c1), Act.Square, *unit)

        def diff(k, off, o0, c0, c1):
            tt(A("df", 1024 * k + c0, 1024 * k + c1), IND(xt, off, o0 + c0, o0 + c1), A(own, c0, c1), Alu.subtract)

        def penalty(bank, big, e, last=False):
            mm(P(bank, 0, 64), blk("idn", big, 128), blk("ee", e), e == 0, last)

        cut = 1024 - SHARE[rnd]
        diff(0, "op", 0, 0, cut)
        if cut < 1024:
            cp(A("gn", cut, 1024), IND(xt, "op", cut, 1024), "s")
            mm(P(3, 0, 1024 - cut), blk("idn", 4, 128), A(own, cut, 1024), True, False)
            mm(P(3, 0, 1024 - cut), blk("idn", 0, 128), A("gn", cut, 1024), False, True)
        cp(A("ft", 0, 1024), P(6, 0, 1024), "s")
        for bank, big in [(0, 2), (1, 3), (2, 3)]:
            penalty(bank, big, 0)
        if cut < 1024:
            act(A("sq", cut, 1024), P(3, 0, 1024 - cut), Act.Square, *unit)
            conv("sq", 0, cut, 1024, 0, True)
        square(0, 0, cut)
        conv("sq", 0, 0, cut, 0, True)
        penalty(0, 2, 1)
        penalty(0, 2, 2, True)
        for c0, c1 in CA:
            diff(1, "oab", 1024, c0, c1)
            square(1, c0, c1)
            conv("sq", 1024, c0, c1, 1, True)
        for c0, c1 in CB:
            diff(2, "oab", 0, c0, c1)
            square(2, c0, c1)
            conv("sq", 2048, c0, c1, 2, True)
        cp(A("abd"), IND("ft", "fcd", 64, 192, 0, 1024), ABD)
        tt(A("ee", 192, 320), A("abd"), A("ld"), Alu.is_equal)
        penalty(1, 3, 2)
        penalty(1, 3, 3, True)
        penalty(2, 3, 1)
        penalty(2, 3, 4, True)
        cp(S1(0), P(0, 0, 64), SMALL)
        tt(S1(1), blk("abd", 0), PD, Alu.subtract)
        tt(Z(0), P(1, 0, 64), S1(0), Alu.is_lt)
        tt(S1(2), P(1, 0, 64), S1(0), Alu.min)
        tt(Z(1), Z(0), S1(1), Alu.mult)
        tt(A("c1", 1, 192, 3), Z(1), PD, Alu.add)
        tt(A("c1", 0, 192, 3), blk("abd", 1), A("c1", 1, 192, 3), Alu.subtract)
        tt(Z(5), P(2, 0, 64), S1(2), Alu.min)
        tt(A("c0", 1, 192, 3), P(2, 0, 64), S1(2), Alu.is_lt)
        ts(A("c1", 2, 192, 3), Z(5), A("thf", 0, 1), Alu.is_ge, 8192.0, Alu.mult)
        chain(A("c2"), A("c0"), A("c1"))
        cp(blk("kb", 0), A("c2", 2, 192, 3))
        partner_row()
        tt(blk("kb", 2), A("c2", 2, 192, 3), blk("kb", 0), Alu.subtract)
        cp(A("m8", 0, 512), IND("t8", "olo", 0, 512), "s")
        partner_column()
        table8("wt", 3, [6, 7], "v")
        cp(A("m8", 512, 1024), IND("t8", "olo", 512, 1024), "s")
        table16(3, [PD])
        cp(blk("ft", 2, 512), P(3), "s")
        for k in range(3):
            conv2(*masked("wt", "ohi", "m8", k), 4)
        for k in range(2):
            cp(blk("m16", k, 512), IND("t16", "vlo", 512 * k, 512 * k + 512), "s")
        tt(S1(3), IND("ft", "fcd", 0, 64), A("idc"), Alu.subtract)
        split(blk("ah", 2), blk("al", 2), S1(3), ON[2][2])
        tt(Z(0), two(4, 0), A("idc"), Alu.is_equal)
        tt(S1(1), two(4, 1), blk("lc", 1), Alu.subtract)
        for k, nm in enumerate(["ah", "al"]):
            tt(blk("thl", k), Z(0), blk(nm, 2), Alu.mult)
        tt(Z(2), Z(0), S1(1), Alu.mult)
        tt(blk("lc", 1), Z(2), blk("lc", 1), Alu.add)
        cp(A("on"), blk("lc", 1))
        for bk in range(2):
            table16(bk, [blk("thl", 0), blk("thl", 1)], range(4 * bk, 4 * bk + 4))
            cp(blk("dtab", bk, 256), P(bk, 256 * bk, 256 * bk + 256), ON[1][bk])
        turns = [to[k] for k in (1, 2, 3, 0)]
        h0 = turns[0][0] // 4

        def ahead(hh):
            cp(blk("gn", hh, 512), IND(xt, "on", 512 * hh, 512 * hh + 512), "s")
            mm(P(6 + hh), blk("idn", 1, 128), blk(own, hh, 512), True, False)
            mm(P(6 + hh), blk("idn", 0, 128), blk("gn", hh, 512), False, True)

        def ahead_out(hh):
            act(blk("uu", hh, 512), P(6 + hh), Act.Identity, [4098.5, 8194.0][rnd])

        def smooth(c0, n):
            tt(A(new, c0, c0 + n), IND(xt, "ov", c0, c0 + n), A("uu", c0, c0 + n), Alu.add)

        def behind(c0, n, bank):
            tt(A("gp", c0, c0 + n), IND("dtab", "vhi", c0, c0 + n), A("m16", c0, c0 + n), Alu.mult)
            conv("gp", 0, c0, c0 + n, bank)
            tt(A("lc", c0 // 16, (c0 + n) // 16), P(bank, c0 // 16, (c0 + n) // 16), A("lc", c0 // 16, (c0 + n) // 16), Alu.add)
            cp(A("ov", c0 // 16, (c0 + n) // 16), A("lc", c0 // 16, (c0 + n) // 16))

        ahead(h0)
        ahead_out(h0)
        ahead(1 - h0)
        ahead_out(1 - h0)
        if rnd == 0:
            for k, (c0, n) in enumerate([(512 * h0, 512), (512 - 512 * h0, 512)]):
                behind(c0, n, 2 + k)
            split(blk("ah", 0), blk("al", 0), blk("lc", 0))
            table16(1, [blk("ah", 0), blk("al", 0)])
            smooth(512 * h0, 256)
            smooth(512 * h0 + 256, 256)
            smooth(512 - 512 * h0, 512)
            table16(0, [blk("lc", 1)])
            for t in range(2):
                cp(blk("ft", t, 512), P(t), "s")
            cp(A("ld"), IND("ft", "fcd", 64, 192, 0, 1024), "a")
            partner_links()
            qs = list(range(4 * h0, 4 * h0 + 4)) + list(range(4 - 4 * h0, 8 - 4 * h0))
            points("xt1", "v16", qs[:6], [2, 6, 2, 6, 0, 2], WHOLE[1], -4100.0)
            partner_lists()
            cp(A("op"), IND("ft", "fcd", 0, 64))
            points("xt1", "v16", qs[6:], [0, 2], WHOLE[1][6:], -4100.0)
            closed()
            prv_place()
        else:
            cp(blk("lo", 2), IND("ft", "fda", 0, 64), "s")
            dma("y", D("dvs"), blk("lo", 2))
            dma("y", D("landv", r), A("lo", 128, 192, None, 16 * r, 16 * r + 16))
            exchange("v")
            home = T.back[:, 128 * r:128 * r + 128]
            def successors(bank, q):
                table16(bank, [blk("lc", 1)])
                cp(blk("ft", 0, 512), P(bank), q)
                cp(blk("lo", 1), IND("ft", "fac", 0, 64, 0, 512), q)
                dma("y", D("dos", None, 1), blk("lo", 1))

            if TAIL == 10:
                successors(4, "s")
                c1 = 128 * turns[0][0]
                behind(c1, 256, 2)
                for c0, n in [(c1 + 256, 768 - c1), (0, c1)]:
                    if n:
                        behind(c0, n, 3 if c0 else 1)
            else:
                for k in range(4):
                    behind(128 * turns[k][0], 256, 2 + k % 2)
            for k in range(4):
                qs, bk = turns[k], [4, 6 + h0, 4, 7 - h0][k]
                c0 = 128 * qs[0]
                smooth(c0, 256)
                mm(P(bk, 0, 256), blk("prm", 1, 128), A(new, c0, c0 + 256))
                if k < 3:
                    cp(A("so", c0, c0 + 256), P(bk, 0, 256), "a", -1025.0)
                    if k < 2 or not JOIN:
                        send(pieces("so", qs[0], qs, home, "br%d" % (k + 1)), [A("lo")] if k == 1 else [])
                else:
                    j = qs.index(mate)
                    cp(blk("so", mate, 128), P(bk, 128 * j, 128 * j + 128), "a", -1025.0)
                    send((pieces("so", to[3][0], to[3], home, "br3") if JOIN else []) + [(mate, near, blk("so", mate, 128), home, "brm")])
                    cp(blk("xo", r, 128), P(bk, 128 - 128 * j, 256 - 128 * j), "a", -1025.0)
                if k == 0:
                    split(blk("ah", 0), blk("al", 0), blk("lc", 0))
                    table16(0, [blk("ah", 0), blk("al", 0)])
                    if TAIL != 10:
                        successors(1, "a")
                    cp(blk("ft", 1, 512), P(0), "a")
                    cp(blk("lo", 0), IND("ft", "fac", 64, 128, 0, 1024), "a")
                    dma("y", D("dos", None, 0), blk("lo", 0))
                    for t in (1, 0):
                        dma("y", D("lando", r, t), A("lo", 64 * t, 64 * t + 64, None, 16 * r, 16 * r + 16))
            exchange("o")

    arrive([blk("back", mate, 128)], "brm", len(near))
    for k in (1, 2, 3):
        arrive([blk("back", q, 128) for q in fr[k]], "br%d" % k, 2 * hf)
    dma("y", X(T.yx[16 * r:16 * r + 16, :]), blk("xo", r, 128))
    dma("y", X(T.yp[:]), D("landv"))
    for j, qs in enumerate([fr[1], fr[2], [mate], fr[3]] if JOIN else [fr[1], [mate], fr[2], fr[3]]):
        cp(A("xo", 128 * qs[0], 128 * qs[-1] + 128), A("back", 128 * qs[0], 128 * qs[-1] + 128))
        for q in qs:
            dma("ys"[q % 2], X(T.yx[16 * q:16 * q + 16, :]), blk("xo", q, 128))
    dma("s", X(T.yn[:]), D("lando", None, 1))
    dma("y", X(T.yv[:]), D("lando", None, 0))

    def meet(a, b):
        if a[5] == b[5] and a[3] % a[5] != b[3] % b[5]:
            return False
        return a[0] == b[0] and a[1] < b[2] and b[1] < a[2] and a[3] < b[4] and b[3] < a[4]

    def follows():
        seen, last = {}, {}
        for i, o in enumerate(ops):
            dep = set()
            for k, wr in [(k, True) for k in o["w"]] + [(k, False) for k in o["r"]]:
                for j, kk, ww in seen.get(k[0], []):
                    bank = k[0].startswith("ps") and (ops[j]["q"] != o["q"] or o["q"] in "pa")
                    if bank or ((wr or ww) and meet(k, kk)):
                        dep.add(j)
            if o["kind"] == "a":
                dep = {o["like"]}
            if o["kind"] in "dr" or o["q"] == "g":
                if o["q"] in last:
                    o["behind"] = last[o["q"]]
                last[o["q"]] = i
            o["dep"] = dep
            for k in o["w"]:
                seen.setdefault(k[0], []).append((i, k, True))
            for k in o["r"]:
                seen.setdefault(k[0], []).append((i, k, False))

    def place(rank, back, LOOK):
        n = len(ops)
        after, left, ready, at, on_q = [[] for _ in ops], [0] * n, [0] * n, [0] * n, [None] * n
        for i, o in enumerate(ops):
            for j in o["dep"] | ({o["behind"]} if "behind" in o else set()):
                a, b = (i, j) if back else (j, i)
                after[a].append(b)
                left[b] += 1
        free, wire, done, bind, begin, latest = {q: 0 for q in Q}, [0], [], [None] * n, [0] * n, {}
        todo = [i for i in range(n) if left[i] == 0]
        while todo:
            can = [(max(ready[i], free.get(q, 0)), i, q) for i in todo for q in (["s", "v"] if ops[i]["q"] == "a" else [ops[i]["q"]])]
            t0, _, q0 = min(can, key=lambda c: c[0])
            due = 1e9
            for t, i, q in sorted([c for c in can if c[2] == q0], key=lambda c: (rank[c[1]], c[1])):
                o = ops[i]
                hold = o["hold"][q] if isinstance(o["hold"], dict) else o["hold"]
                if t <= t0 + LOOK and t + hold <= due + SLACK:
                    break
                if t > t0 + LOOK and o["q"] not in ("a", None):
                    due = min(due, t)
            else:
                free[q0] = due
                continue
            todo.remove(i)
            done.append(i)
            on_q[i], begin[i] = q, t
            if t > ready[i]:
                bind[i] = latest.get(q)
            latest[q] = i
            if back and "wire" in o:
                wire[0] = t = max(t, wire[0]) + o["wire"]
            if q is not None:
                free[q] = t + hold
            end = t + hold
            if not back:
                end += o["flight"]
                if "wire" in o:
                    wire[0] = end = max(end, wire[0]) + o["wire"]
            at[i] = end
            for j in after[i]:
                e = ops[j]
                wake = 0 if q == "p" == e["q"] else WAKE
                if back:
                    due = end + wake + (e["flight"] if j in o["dep"] else 0)
                else:
                    due = end + wake if i in e["dep"] else t
                if due > ready[j]:
                    ready[j], bind[j] = due, i
                left[j] -= 1
                if left[j] == 0:
                    todo.append(j)
        return max(at), done, on_q, [-t for t in at], bind, begin

    follows()
    above = []
    for o in ops:
        m = 0
        for j in o["dep"]:
            m |= above[j]
        o["dep"] = {j for j in o["dep"] if not m >> j & 1}
        above.append(m | sum(1 << j for j in o["dep"]))
    best = tried = place(list(range(len(ops))), False, LOOKS[0])
    for look in LOOKS:
        tried = place(place(best[3], True, look)[3], False, look)
        best = min(best, tried, key=lambda b: b[0])
    for i, o in enumerate(ops):
        o["any"] = o["hold"] if o["q"] == "a" else None
        o["q"] = best[2][i]
        o["hold"] = o["hold"][o["q"]] if isinstance(o["hold"], dict) else o["hold"]

    def replay(order, wake, more):
        free, last, end, bind, wire = {}, {}, {}, {}, 0
        for i in order:
            o = ops[i]
            q = o["q"]
            t, bind[i] = (free.get(q, 0), last.get(q)) if q else (0, None)
            for j in o["dep"]:
                e = end[j] + (0 if q == "p" == ops[j]["q"] else wake)
                if e > t:
                    t, bind[i] = e, j
            free[q], last[q] = t + o["hold"] + more.get(q, 0), i
            end[i] = free[q] + o["flight"]
            if "wire" in o:
                wire = end[i] = max(end[i], wire) + o["wire"]
        return max(end.values()) + EARLY * sum(end.values()), bind, max(end, key=end.get)

    def length(order):
        return sum(replay(order, wake, more)[0] for wake, more in SPREAD)

    order, now = best[1], length(best[1])
    for k in range(SWEEPS):
        _, bind, i = replay(order, *SPREAD[k % len(SPREAD)])
        while bind[i] is not None:
            j = bind[i]
            o = ops[i]
            if o["any"]:
                was = o["q"]
                o["q"] = "s" if was == "v" else "v"
                o["hold"] = o["any"][o["q"]]
                if length(order) < now:
                    now = length(order)
                else:
                    o["q"], o["hold"] = was, o["any"][was]
            if ops[i]["q"] == ops[j]["q"] and ops[i]["q"] in "vsp" and ops[i]["kind"] == "c" == ops[j]["kind"] and j not in ops[i]["dep"]:
                a, b = order.index(j), order.index(i)
                tied = {j}
                for x in order[a + 1:b + 1]:
                    if ops[x]["dep"] & tied or ops[x].get("behind") in tied:
                        tied.add(x)
                if i not in tied:
                    other = order[:a] + [x for x in order[a:b + 1] if x not in tied] + [x for x in order[a:b + 1] if x in tied] + order[b + 1:]
                    if length(other) < now:
                        order, now = other, length(other)
            i = j
    ops = [ops[i] for i in order]
    clock = {q: {} for q in Q}
    seen = {}
    for i, o in enumerate(ops):
        o["waits"], o["sig"] = [], o["kind"] != "c"
        o["lane"] = o["q"] if o["kind"] == "c" else o["sem"]
        if o["kind"] != "a":
            need = {}
            for k, wr in [(k, True) for k in o["w"]] + [(k, False) for k in o["r"]]:
                for j, kk, ww in seen.get(k[0], []):
                    e = ops[j]
                    if e["q"] == "p" and o["q"] == "p":
                        continue
                    bank = k[0].startswith("ps") and e["q"] != o["q"]
                    if bank or ((wr or ww) and meet(k, kk)):
                        need[e["lane"]] = max(need.get(e["lane"], -1), j)
            ck = clock[o["q"]]
            for j in sorted(need.values(), reverse=True):
                e = ops[j]
                if ck.get(e["lane"], -1) < j:
                    o["waits"].append(j)
                    e["sig"] = True
                    for ln, v in e["clk"].items():
                        if ck.get(ln, -1) < v:
                            ck[ln] = v
            o["clk"] = dict(ck)
        else:
            o["clk"] = {}
        o["clk"][o["lane"]] = i
        for k in o["w"]:
            seen.setdefault(k[0], []).append((i, k, True))
        for k in o["r"]:
            seen.setdefault(k[0], []).append((i, k, False))
    count, waited = {}, {}
    for o in ops:
        if o["kind"] == "c":
            o["sem"], o["n"] = "c" + o["q"], 1
        if o["sig"]:
            count[o["sem"]] = count.get(o["sem"], 0) + o["n"]
            o["at"] = count[o["sem"]]
    for o in ops:
        if o["kind"] == "a":
            continue
        for j in o["waits"]:
            e = ops[j]
            Q[o["q"]].wait_ge(T.sem[e["sem"]], e["at"])
            waited[e["sem"]] = max(waited.get(e["sem"], 0), e["at"])
        ins = o["fn"][o["q"]]() if isinstance(o["fn"], dict) else o["fn"]()
        if o["sig"] and o["kind"] != "r":
            ins.then_inc(T.sem[o["sem"]], o["n"])
    for sem in count:
        if waited.get(sem, 0) < count[sem]:
            g.wait_ge(T.sem[sem], count[sem])
